import numpy as np
import ml_dtypes


def mxq(x, axis, fmt="e4m3"):
    dtype, down = {"e4m3": (ml_dtypes.float8_e4m3fn, 7), "e5m2": (ml_dtypes.float8_e5m2, 14)}[fmt]
    v = np.moveaxis(np.asarray(x, np.float32).astype(ml_dtypes.bfloat16).astype(np.float64), axis, -1)
    blocks = v.reshape(v.shape[:-1] + (-1, 32))
    amax = np.abs(blocks).max(-1, keepdims=True)
    byte = np.maximum(np.where(amax > 0, np.frexp(amax)[1] - 1 + 127, 0) - down, 1)
    scale = np.exp2(byte - 127.0)
    codes = (blocks / scale).astype(np.float32).astype(dtype).astype(np.float64)
    return np.moveaxis((codes * scale).reshape(v.shape), -1, axis)


WIDE = False


def mx_kscale(k):
    if not WIDE:
        return np.ones(k)
    levels = np.array([10, -10, 5, -5, 0])
    if k % 512:
        return np.exp2(np.random.permutation(np.resize(levels, k // 32))).repeat(32)
    a = np.empty((k // 512, 16))
    for p in range(k // 512):
        a[p, :8] = np.random.permutation(np.resize(levels, 8))
        for g in range(8):
            far = levels[np.abs(levels - a[p, g]) >= 10]
            a[p, g + 8] = far[np.random.randint(len(far))]
    return np.exp2(a.ravel()).repeat(32)


def f64(x):
    return np.asarray(x).astype(np.float64)


def striped(idx):
    return np.tile(idx.reshape(-1, 16).T, (8, 1)).astype(np.uint16)


def unstriped(offs):
    return offs[:16].T.reshape(-1).astype(np.int64)


def striped8(idx):
    return np.concatenate([x.reshape(-1, 16).T for x in idx]).astype(np.uint16)


def runs(offs, k):
    lists = np.stack([offs[16 * r : 16 * r + 16].T.reshape(-1) for r in range(8)]).astype(np.int64)
    return lists[np.arange(k) % 512 // 64]


def pack_weight(w):
    k, n = w.shape
    w = f64(np.asarray(w, np.float32).astype(ml_dtypes.bfloat16)).reshape(k // 32, 32, n)
    amax = np.abs(w).max(1)
    byte = np.clip(np.where(amax > 0, np.frexp(amax)[1] - 1 + 127 - 7, 1), 1, 254)
    scaled = (w * np.exp2(127.0 - byte)[:, None, :]).reshape(k, n).astype(np.float32)
    words = np.ascontiguousarray(scaled.reshape(k // 512, 128, 4, n).transpose(0, 1, 3, 2)).astype(ml_dtypes.float8_e4m3fn).view(np.uint8)
    return words, np.ascontiguousarray(byte.astype(np.uint8).reshape(k // 512, 16, n))


def unpack_weight(words, scales):
    g, p, n, _ = words.shape
    vals = np.ascontiguousarray(words).view(ml_dtypes.float8_e4m3fn).astype(np.float64) * np.repeat(np.exp2(scales.astype(np.float64) - 127.0), 8, axis=1)[..., None]
    return vals.transpose(0, 1, 3, 2).reshape(g * 512, n)


K, T, S, N, H, U = 512, 2048, 512, 512, 512, 1024


def setup_inputs():
    n = np.random.standard_normal
    s = mx_kscale(K)[:, None]
    u = mx_kscale(H)
    packed_xT = pack_weight(n((K, T)) * s)
    return {
        "x_words": packed_xT[0],
        "x_scales": packed_xT[1],
        "w1": (n((K, H)) / np.sqrt(K) / s * u).astype(np.float32),
        "gain": np.random.uniform(0.3, 1.5, (H, U)).astype(np.float32),
        "w2": (n((K, N)) / np.sqrt(2 * K) / s).astype(np.float32),
        "w3": (n((H, N)) / np.sqrt(2 * H) / u[:, None]).astype(np.float32),
        "offs": striped(np.random.permutation(T)[:S]),
        "ad": striped8(np.stack([np.random.permutation(U)[(U * np.random.uniform(0, 1, S) ** 4).astype(np.int64)] for _ in range(8)])),
    }


def reference(x_words, x_scales, w1, gain, w2, w3, offs, ad):
    xq = unpack_weight(x_words, x_scales)[:, unstriped(offs)]
    h = mxq(f64(w1), 0, "e4m3").T @ xq
    z = h * (f64(gain)[np.arange(H)[:, None], runs(ad, H)])
    return mxq(f64(w2), 0, "e4m3").T @ xq + mxq(f64(w3), 0, "e4m3").T @ mxq(z, 0, "e4m3")

@@ -1,0 +1,142 @@
+from contextlib import ExitStack
+
+import concourse.mybir as mybir
+
+K, T, S, N, H, U = 512, 2048, 512, 512, 512, 1024
+FLOPS = 3 * 2 * 512 * 512 * 512
+
+F32 = mybir.dt.float32
+BF16 = mybir.dt.bfloat16
+I32 = mybir.dt.int32
+U32 = mybir.dt.uint32
+U16 = mybir.dt.uint16
+U8 = mybir.dt.uint8
+FP8X4 = mybir.dt.float8_e4m3fn_x4
+MULT = mybir.AluOpType.mult
+
+P = 128
+PACK = 4
+BLK = 128
+
+
+def tile_picked_slorah_none_p_kernel(tc, x_words, x_scales, w1, gain, w2, w3, offs, ad, out):
+    nc = tc.nc
+    with ExitStack() as ctx:
+        keep = ctx.enter_context(tc.tile_pool(name="keep", bufs=1))
+        psum = ctx.enter_context(tc.psum_pool(name="psum", bufs=1))
+
+        offs_sb = keep.tile([P, S // 16], U16, name="offs_sb")
+        ad_sb = keep.tile([P, S // 16], U16, name="ad_sb")
+        x_table = keep.tile([P, T], U32, name="x_table", align_bytes=64)
+        xs_table = keep.tile([P, T], U8, name="xs_table", align_bytes=64)
+        gain_table = [keep.tile([P, U], F32, name="gain_table%d" % t, align_bytes=64) for t in range(PACK)]
+        raw = {n: keep.tile([P, PACK, 512], F32, name=n + "_raw", align_bytes=64) for n in ("w1", "w2", "w3")}
+        grouped = {n: keep.tile([P, 512 * PACK], BF16, name=n + "_grouped", align_bytes=64) for n in ("w1", "w2", "w3", "z")}
+        codes = {n: keep.tile([P, 512], U32, name=n + "_codes", align_bytes=64) for n in ("w1", "w2", "w3", "z", "x")}
+        scales = {n: keep.tile([P, 512], U8, name=n + "_scales", align_bytes=64) for n in ("w1", "w2", "w3", "z", "x")}
+        picked_gain = keep.tile([P, PACK, S], F32, name="picked_gain", align_bytes=64)
+
+        gain_rows = gain.rearrange("(p t) u -> p t u", t=PACK)
+
+        def load_weight(name, w):
+            nc.sync.dma_start(raw[name][:], w.rearrange("(p j) n -> p j n", j=PACK))
+
+        def load_gain(t):
+            nc.sync.dma_start(gain_table[t][:], gain_rows[:, t, :])
+
+        def gather_gain(t):
+            nc.vector.tensor_copy(picked_gain[:, t, :], gain_table[t][:].indirect(ad_sb[:]))
+
+        def quantize(name, c0, c1):
+            nc.vector.quantize_mx(
+                out=codes[name][:, c0:c1].bitcast(FP8X4),
+                scales=scales[name][:, c0:c1],
+                in_=grouped[name][:, PACK * c0 : PACK * c1],
+            )
+
+        def interleave(copy, name, c0, c1):
+            copy(
+                grouped[name][:, PACK * c0 : PACK * c1].rearrange("p (c i j) -> p c j i", i=4, j=PACK),
+                raw[name][:, :, c0:c1].rearrange("p j (c i) -> p c j i", i=4),
+            )
+
+        def product(acc, lhs, m, rhs, c0, c1, start, stop):
+            cols = slice(m * BLK, (m + 1) * BLK)
+            nc.tensor.matmul_mx(
+                out=acc,
+                lhsT=codes[lhs][:, cols].bitcast(FP8X4),
+                lhsT_scale=scales[lhs][:, cols],
+                rhs=codes[rhs][:, c0:c1].bitcast(FP8X4),
+                rhs_scale=scales[rhs][:, c0:c1],
+                start=start,
+                stop=stop,
+            )
+
+        nc.vector.memset(xs_table[:].bitcast(I32), 0)
+        load_weight("w1", w1)
+        nc.sync.dma_start(offs_sb[:], offs)
+        nc.sync.dma_start(ad_sb[:], ad)
+        for q in range(4):
+            nc.scalar.dma_start(xs_table[32 * q : 32 * q + 4, :].bitcast(I32), x_scales[0, 4 * q : 4 * q + 4, :].bitcast(I32))
+        load_gain(0)
+        nc.sync.dma_start(x_table[:].bitcast(I32), x_words[0].rearrange("p n t -> p (n t)").bitcast(I32))
+        for t in range(1, PACK):
+            load_gain(t)
+        load_weight("w2", w2)
+        load_weight("w3", w3)
+
+        nc.vector.tensor_copy(scales["x"][:], xs_table[:].indirect(offs_sb[:]))
+        nc.scalar.copy(
+            grouped["w1"][:].rearrange("p (t m j) -> p m j t", t=PACK, j=PACK),
+            raw["w1"][:].rearrange("p j (m t) -> p m j t", t=PACK),
+        )
+        gather_gain(0)
+        quantize("w1", 0, H)
+        nc.vector.tensor_copy(codes["x"][:], x_table[:].indirect(offs_sb[:]))
+        for t in range(1, PACK):
+            gather_gain(t)
+
+        chunks = S // BLK
+        h = [psum.tile([P, PACK, BLK], F32, name="h%d" % c) for c in range(chunks)]
+        for c in range(chunks):
+            for t in range(PACK):
+                product(h[c][:, t, :], "w1", t, "x", c * BLK, (c + 1) * BLK, True, True)
+
+        def scale_hidden(c):
+            cols = slice(c * BLK, (c + 1) * BLK)
+            nc.vector.tensor_tensor(
+                grouped["z"][:, PACK * c * BLK : PACK * (c + 1) * BLK].rearrange("p (c i t) -> p c t i", i=4, t=PACK),
+                h[c][:].rearrange("p t (c i) -> p c t i", i=4),
+                picked_gain[:, :, cols].rearrange("p t (c i) -> p c t i", i=4),
+                MULT,
+            )
+
+        interleave(nc.scalar.copy, "w2", 0, 256)
+        interleave(nc.scalar.copy, "w2", 256, 512)
+        scale_hidden(0)
+        scale_hidden(1)
+        scale_hidden(2)
+        quantize("z", 0, 256)
+        scale_hidden(3)
+        quantize("w2", 0, 256)
+        quantize("z", 256, 512)
+        quantize("w2", 256, 512)
+
+        acc = [psum.tile([P, S], F32, name="acc%d" % m) for m in range(N // BLK)]
+        for m in range(N // BLK):
+            product(acc[m][:], "w2", m, "x", 0, S, True, False)
+
+        interleave(nc.scalar.copy, "w3", 0, 128)
+        interleave(nc.vector.tensor_copy, "w3", 256, 512)
+        interleave(nc.scalar.copy, "w3", 128, 256)
+        quantize("w3", 0, 128)
+        quantize("w3", 256, 512)
+        quantize("w3", 128, 256)
+        for i, m in enumerate((0, 2, 3, 1)):
+            product(acc[m][:], "w3", m, "z", 0, S, False, True)
+            result = keep.tile([P, S], F32, name="result%d" % m)
+            if i % 2 == 0:
+                nc.scalar.copy(result[:], acc[m][:])
+            else:
+                nc.vector.tensor_copy(result[:], acc[m][:])
+            nc.sync.dma_start(out[m * BLK : (m + 1) * BLK, :], result[:])

@@ -31,7 +31,10 @@ def tile_picked_slorah_none_p_kernel(tc, x_words, x_scales, w1, gain, w2, w3, of
         xs_table = keep.tile([P, T], U8, name="xs_table", align_bytes=64)
         gain_table = [keep.tile([P, U], F32, name="gain_table%d" % t, align_bytes=64) for t in range(PACK)]
         raw = {n: keep.tile([P, PACK, 512], F32, name=n + "_raw", align_bytes=64) for n in ("w1", "w2", "w3")}
-        grouped = {n: keep.tile([P, 512 * PACK], BF16, name=n + "_grouped", align_bytes=64) for n in ("w1", "w2", "w3", "z")}
+        grouped = {n: keep.tile([P, 512 * PACK], BF16, name=n + "_grouped", align_bytes=64) for n in ("w1", "w3")}
+        shared = keep.tile([P, 1536 + 2048], BF16, name="shared", align_bytes=64)
+        grouped["z"] = shared[:, 0:2048]
+        grouped["w2"] = shared[:, 1536:3584]
         codes = {n: keep.tile([P, 512], U32, name=n + "_codes", align_bytes=64) for n in ("w1", "w2", "w3", "z", "x")}
         scales = {n: keep.tile([P, 512], U8, name=n + "_scales", align_bytes=64) for n in ("w1", "w2", "w3", "z", "x")}
         picked_gain = keep.tile([P, PACK, S], F32, name="picked_gain", align_bytes=64)
@@ -73,28 +76,31 @@ def tile_picked_slorah_none_p_kernel(tc, x_words, x_scales, w1, gain, w2, w3, of
             )
 
         nc.vector.memset(xs_table[:].bitcast(I32), 0)
-        load_weight("w1", w1)
-        nc.sync.dma_start(offs_sb[:], offs)
+        load_gain(0)
         nc.sync.dma_start(ad_sb[:], ad)
+        nc.sync.dma_start(offs_sb[:], offs)
         for q in range(4):
             nc.scalar.dma_start(xs_table[32 * q : 32 * q + 4, :].bitcast(I32), x_scales[0, 4 * q : 4 * q + 4, :].bitcast(I32))
-        load_gain(0)
+        load_weight("w1", w1)
+        load_gain(1)
+        load_gain(2)
         nc.sync.dma_start(x_table[:].bitcast(I32), x_words[0].rearrange("p n t -> p (n t)").bitcast(I32))
-        for t in range(1, PACK):
-            load_gain(t)
+        load_gain(3)
         load_weight("w2", w2)
         load_weight("w3", w3)
 
+        gather_gain(0)
         nc.vector.tensor_copy(scales["x"][:], xs_table[:].indirect(offs_sb[:]))
         nc.scalar.copy(
             grouped["w1"][:].rearrange("p (t m j) -> p m j t", t=PACK, j=PACK),
             raw["w1"][:].rearrange("p j (m t) -> p m j t", t=PACK),
         )
-        gather_gain(0)
+        gather_gain(1)
+        gather_gain(2)
         quantize("w1", 0, H)
-        nc.vector.tensor_copy(codes["x"][:], x_table[:].indirect(offs_sb[:]))
-        for t in range(1, PACK):
-            gather_gain(t)
+        for half in range(2):
+            nc.vector.tensor_copy(codes["x"][:, half * 256 : (half + 1) * 256], x_table[:].indirect(offs_sb[:, half * 16 : (half + 1) * 16]))
+        gather_gain(3)
 
         chunks = S // BLK
         h = [psum.tile([P, PACK, BLK], F32, name="h%d" % c) for c in range(chunks)]
@@ -113,30 +119,35 @@ def tile_picked_slorah_none_p_kernel(tc, x_words, x_scales, w1, gain, w2, w3, of
 
         interleave(nc.scalar.copy, "w2", 0, 256)
         interleave(nc.scalar.copy, "w2", 256, 512)
+        acc = [psum.tile([P, S], F32, name="acc%d" % m) for m in range(N // BLK)]
+        result = [keep.tile([P, S], F32, name="result%d" % m) for m in range(N // BLK)]
+
+        def finish(m, copy):
+            product(acc[m][:], "w3", m, "z", 0, S, False, True)
+            copy(result[m][:], acc[m][:])
+            nc.sync.dma_start(out[m * BLK : (m + 1) * BLK, :], result[m][:])
+
         scale_hidden(0)
         scale_hidden(1)
         scale_hidden(2)
         quantize("z", 0, 256)
-        scale_hidden(3)
         quantize("w2", 0, 256)
+        product(acc[0][:], "w2", 0, "x", 0, S, True, False)
+        product(acc[1][:], "w2", 1, "x", 0, S, True, False)
+        scale_hidden(3)
         quantize("z", 256, 512)
-        quantize("w2", 256, 512)
-
-        acc = [psum.tile([P, S], F32, name="acc%d" % m) for m in range(N // BLK)]
-        for m in range(N // BLK):
-            product(acc[m][:], "w2", m, "x", 0, S, True, False)
-
         interleave(nc.scalar.copy, "w3", 0, 128)
-        interleave(nc.vector.tensor_copy, "w3", 256, 512)
         interleave(nc.scalar.copy, "w3", 128, 256)
+        interleave(nc.scalar.copy, "w3", 256, 384)
         quantize("w3", 0, 128)
-        quantize("w3", 256, 512)
+        finish(0, nc.scalar.copy)
+        interleave(nc.vector.tensor_copy, "w3", 384, 512)
         quantize("w3", 128, 256)
-        for i, m in enumerate((0, 2, 3, 1)):
-            product(acc[m][:], "w3", m, "z", 0, S, False, True)
-            result = keep.tile([P, S], F32, name="result%d" % m)
-            if i % 2 == 0:
-                nc.scalar.copy(result[:], acc[m][:])
-            else:
-                nc.vector.tensor_copy(result[:], acc[m][:])
-            nc.sync.dma_start(out[m * BLK : (m + 1) * BLK, :], result[:])
+        quantize("w2", 256, 512)
+        product(acc[3][:], "w2", 3, "x", 0, S, True, False)
+        product(acc[2][:], "w2", 2, "x", 0, S, True, False)
+        quantize("w3", 384, 512)
+        quantize("w3", 256, 384)
+        finish(1, nc.vector.tensor_copy)
+        finish(3, nc.scalar.copy)
+        finish(2, nc.vector.tensor_copy)

@@ -17,6 +17,7 @@ MULT = mybir.AluOpType.mult
 P = 128
 PACK = 4
 BLK = 128
+FRONT = 3 * BLK
 
 
 def tile_picked_slorah_none_p_kernel(tc, x_words, x_scales, w1, gain, w2, w3, offs, ad, out):
@@ -25,24 +26,29 @@ def tile_picked_slorah_none_p_kernel(tc, x_words, x_scales, w1, gain, w2, w3, of
         keep = ctx.enter_context(tc.tile_pool(name="keep", bufs=1))
         psum = ctx.enter_context(tc.psum_pool(name="psum", bufs=1))
 
+        def sbuf(name, shape, dtype):
+            return keep.tile([P] + shape, dtype, name=name, align_bytes=64)
+
         offs_sb = keep.tile([P, S // 16], U16, name="offs_sb")
         ad_sb = keep.tile([P, S // 16], U16, name="ad_sb")
-        x_table = keep.tile([P, T], U32, name="x_table", align_bytes=64)
-        xs_table = keep.tile([P, T], U8, name="xs_table", align_bytes=64)
-        gain_table = [keep.tile([P, U], F32, name="gain_table%d" % t, align_bytes=64) for t in range(PACK)]
-        raw = {n: keep.tile([P, PACK, 512], F32, name=n + "_raw", align_bytes=64) for n in ("w1", "w2", "w3")}
-        grouped = {n: keep.tile([P, 512 * PACK], BF16, name=n + "_grouped", align_bytes=64) for n in ("w1", "w3")}
-        shared = keep.tile([P, 1536 + 2048], BF16, name="shared", align_bytes=64)
-        grouped["z"] = shared[:, 0:2048]
-        grouped["w2"] = shared[:, 1536:3584]
-        codes = {n: keep.tile([P, 512], U32, name=n + "_codes", align_bytes=64) for n in ("w1", "w2", "w3", "z", "x")}
-        scales = {n: keep.tile([P, 512], U8, name=n + "_scales", align_bytes=64) for n in ("w1", "w2", "w3", "z", "x")}
-        picked_gain = keep.tile([P, PACK, S], F32, name="picked_gain", align_bytes=64)
+        x_table = sbuf("x_table", [T], U32)
+        xs_table = sbuf("xs_table", [T], U8)
+        gain_table = [sbuf("gain_table%d" % t, [U], F32) for t in range(PACK)]
+        picked_gain = sbuf("picked_gain", [PACK, S], F32)
+        widths = {"w1": H, "w2": FRONT, "w3": FRONT, "w2_back": BLK, "w3_back": BLK}
+        raw = {n: sbuf(n + "_raw", [PACK, w], F32) for n, w in widths.items()}
+        widths = {"w1": H, "w2": FRONT, "w3": FRONT, "back": 2 * BLK, "z": S, "x": S}
+        codes = {n: sbuf(n + "_codes", [w], U32) for n, w in widths.items()}
+        scales = {n: sbuf(n + "_scales", [w], U8) for n, w in widths.items()}
+        grouped = {n: sbuf(n + "_grouped", [PACK * widths[n]], BF16) for n in ("w1", "w3", "back")}
+        shared = sbuf("shared", [PACK * (S - BLK + FRONT)], BF16)
+        grouped["z"] = shared[:, 0 : PACK * S]
+        grouped["w2"] = shared[:, PACK * (S - BLK) : PACK * (S - BLK + FRONT)]
 
         gain_rows = gain.rearrange("(p t) u -> p t u", t=PACK)
 
-        def load_weight(name, w):
-            nc.sync.dma_start(raw[name][:], w.rearrange("(p j) n -> p j n", j=PACK))
+        def load_weight(name, w, c0, c1):
+            nc.sync.dma_start(raw[name][:], w.rearrange("(p j) n -> p j n", j=PACK)[:, :, c0:c1])
 
         def load_gain(t):
             nc.sync.dma_start(gain_table[t][:], gain_rows[:, t, :])
@@ -50,17 +56,17 @@ def tile_picked_slorah_none_p_kernel(tc, x_words, x_scales, w1, gain, w2, w3, of
         def gather_gain(t):
             nc.vector.tensor_copy(picked_gain[:, t, :], gain_table[t][:].indirect(ad_sb[:]))
 
-        def quantize(name, c0, c1):
+        def quantize(name, b0, b1):
             nc.vector.quantize_mx(
-                out=codes[name][:, c0:c1].bitcast(FP8X4),
-                scales=scales[name][:, c0:c1],
-                in_=grouped[name][:, PACK * c0 : PACK * c1],
+                out=codes[name][:, b0 * BLK : b1 * BLK].bitcast(FP8X4),
+                scales=scales[name][:, b0 * BLK : b1 * BLK],
+                in_=grouped[name][:, PACK * b0 * BLK : PACK * b1 * BLK],
             )
 
-        def interleave(copy, name, c0, c1):
+        def interleave(copy, dst, d0, src, b0, b1):
             copy(
-                grouped[name][:, PACK * c0 : PACK * c1].rearrange("p (c i j) -> p c j i", i=4, j=PACK),
-                raw[name][:, :, c0:c1].rearrange("p j (c i) -> p c j i", i=4),
+                grouped[dst][:, PACK * d0 * BLK : PACK * (d0 + b1 - b0) * BLK].rearrange("p (c i j) -> p c j i", i=4, j=PACK),
+                raw[src][:, :, b0 * BLK : b1 * BLK].rearrange("p j (c i) -> p c j i", i=4),
             )
 
         def product(acc, lhs, m, rhs, c0, c1, start, stop):
@@ -76,18 +82,20 @@ def tile_picked_slorah_none_p_kernel(tc, x_words, x_scales, w1, gain, w2, w3, of
             )
 
         nc.vector.memset(xs_table[:].bitcast(I32), 0)
-        load_gain(0)
         nc.sync.dma_start(ad_sb[:], ad)
         nc.sync.dma_start(offs_sb[:], offs)
-        for q in range(4):
-            nc.scalar.dma_start(xs_table[32 * q : 32 * q + 4, :].bitcast(I32), x_scales[0, 4 * q : 4 * q + 4, :].bitcast(I32))
-        load_weight("w1", w1)
+        load_gain(0)
+        for r in range(4):
+            nc.sync.dma_start(xs_table[r:P:32, :].bitcast(I32), x_scales[0, r:16:4, :].bitcast(I32))
+        load_weight("w1", w1, 0, H)
         load_gain(1)
         load_gain(2)
         nc.sync.dma_start(x_table[:].bitcast(I32), x_words[0].rearrange("p n t -> p (n t)").bitcast(I32))
         load_gain(3)
-        load_weight("w2", w2)
-        load_weight("w3", w3)
+        load_weight("w2", w2, 0, FRONT)
+        load_weight("w3", w3, 0, FRONT)
+        load_weight("w2_back", w2, FRONT, N)
+        load_weight("w3_back", w3, FRONT, N)
 
         gather_gain(0)
         nc.vector.tensor_copy(scales["x"][:], xs_table[:].indirect(offs_sb[:]))
@@ -97,7 +105,7 @@ def tile_picked_slorah_none_p_kernel(tc, x_words, x_scales, w1, gain, w2, w3, of
         )
         gather_gain(1)
         gather_gain(2)
-        quantize("w1", 0, H)
+        quantize("w1", 0, 4)
         for half in range(2):
             nc.vector.tensor_copy(codes["x"][:, half * 256 : (half + 1) * 256], x_table[:].indirect(offs_sb[:, half * 16 : (half + 1) * 16]))
         gather_gain(3)
@@ -108,46 +116,46 @@ def tile_picked_slorah_none_p_kernel(tc, x_words, x_scales, w1, gain, w2, w3, of
             for t in range(PACK):
                 product(h[c][:, t, :], "w1", t, "x", c * BLK, (c + 1) * BLK, True, True)
 
-        def scale_hidden(c):
+        def scale_hidden(c, engine, hidden):
             cols = slice(c * BLK, (c + 1) * BLK)
-            nc.vector.tensor_tensor(
+            engine.tensor_tensor(
                 grouped["z"][:, PACK * c * BLK : PACK * (c + 1) * BLK].rearrange("p (c i t) -> p c t i", i=4, t=PACK),
-                h[c][:].rearrange("p t (c i) -> p c t i", i=4),
+                hidden[:].rearrange("p t (c i) -> p c t i", i=4),
                 picked_gain[:, :, cols].rearrange("p t (c i) -> p c t i", i=4),
                 MULT,
             )
 
-        interleave(nc.scalar.copy, "w2", 0, 256)
-        interleave(nc.scalar.copy, "w2", 256, 512)
         acc = [psum.tile([P, S], F32, name="acc%d" % m) for m in range(N // BLK)]
-        result = [keep.tile([P, S], F32, name="result%d" % m) for m in range(N // BLK)]
+        result = [sbuf("result%d" % m, [S], F32) for m in range(N // BLK)]
 
-        def finish(m, copy):
-            product(acc[m][:], "w3", m, "z", 0, S, False, True)
+        def finish(m, lhs, b, copy):
+            product(acc[m][:], lhs, b, "z", 0, S, False, True)
             copy(result[m][:], acc[m][:])
             nc.sync.dma_start(out[m * BLK : (m + 1) * BLK, :], result[m][:])
 
-        scale_hidden(0)
-        scale_hidden(1)
-        scale_hidden(2)
-        quantize("z", 0, 256)
-        quantize("w2", 0, 256)
+        interleave(nc.scalar.copy, "w2", 0, "w2", 0, 2)
+        interleave(nc.scalar.copy, "w2", 2, "w2", 2, 3)
+        scale_hidden(0, nc.vector, h[0])
+        scale_hidden(1, nc.vector, h[1])
+        scale_hidden(2, nc.vector, h[2])
+        quantize("z", 0, 2)
+        quantize("w2", 0, 2)
         product(acc[0][:], "w2", 0, "x", 0, S, True, False)
         product(acc[1][:], "w2", 1, "x", 0, S, True, False)
-        scale_hidden(3)
-        quantize("z", 256, 512)
-        interleave(nc.scalar.copy, "w3", 0, 128)
-        interleave(nc.scalar.copy, "w3", 128, 256)
-        interleave(nc.scalar.copy, "w3", 256, 384)
-        quantize("w3", 0, 128)
-        finish(0, nc.scalar.copy)
-        interleave(nc.vector.tensor_copy, "w3", 384, 512)
-        quantize("w3", 128, 256)
-        quantize("w2", 256, 512)
-        product(acc[3][:], "w2", 3, "x", 0, S, True, False)
+        scale_hidden(3, nc.vector, h[3])
+        for b in range(3):
+            interleave(nc.scalar.copy, "w3", b, "w3", b, b + 1)
+        quantize("w3", 0, 1)
+        quantize("z", 2, 4)
+        finish(0, "w3", 0, nc.scalar.copy)
+        quantize("w3", 1, 2)
+        finish(1, "w3", 1, nc.scalar.copy)
+        quantize("w2", 2, 3)
         product(acc[2][:], "w2", 2, "x", 0, S, True, False)
-        quantize("w3", 384, 512)
-        quantize("w3", 256, 384)
-        finish(1, nc.vector.tensor_copy)
-        finish(3, nc.scalar.copy)
-        finish(2, nc.vector.tensor_copy)
+        interleave(nc.vector.tensor_copy, "back", 0, "w2_back", 0, 1)
+        interleave(nc.vector.tensor_copy, "back", 1, "w3_back", 0, 1)
+        quantize("w3", 2, 3)
+        finish(2, "w3", 2, nc.scalar.copy)
+        quantize("back", 0, 2)
+        product(acc[3][:], "back", 0, "x", 0, S, True, False)
+        finish(3, "back", 1, nc.vector.tensor_copy)

@@ -17,7 +17,7 @@ MULT = mybir.AluOpType.mult
 P = 128
 PACK = 4
 BLK = 128
-FRONT = 3 * BLK
+HALF = 256
 
 
 def tile_picked_slorah_none_p_kernel(tc, x_words, x_scales, w1, gain, w2, w3, offs, ad, out):
@@ -35,38 +35,35 @@ def tile_picked_slorah_none_p_kernel(tc, x_words, x_scales, w1, gain, w2, w3, of
         xs_table = sbuf("xs_table", [T], U8)
         gain_table = [sbuf("gain_table%d" % t, [U], F32) for t in range(PACK)]
         picked_gain = sbuf("picked_gain", [PACK, S], F32)
-        widths = {"w1": H, "w2": FRONT, "w3": FRONT, "w2_back": BLK, "w3_back": BLK}
-        raw = {n: sbuf(n + "_raw", [PACK, w], F32) for n, w in widths.items()}
-        widths = {"w1": H, "w2": FRONT, "w3": FRONT, "back": 2 * BLK, "z": S, "x": S}
+        pieces = {"w1": (w1, 0, H), "w2a": (w2, 0, 256), "w3a": (w3, 0, 256), "w2b": (w2, 256, 512), "w3c": (w3, 256, 384), "w3d": (w3, 384, 512)}
+        raw = {n: sbuf(n + "_raw", [PACK, c1 - c0], F32) for n, (w, c0, c1) in pieces.items() if n != "w3a"}
+        shared = sbuf("shared", [HALF + PACK * 256], F32)
+        raw["w3a"] = shared[:, HALF:].rearrange("p (j n) -> p j n", j=PACK)
+        widths = {"w1": H, "w2a": 256, "w3a": 256, "w2b": 256, "w3c": BLK, "w3d": BLK, "za": HALF, "zb": HALF, "x": S}
         codes = {n: sbuf(n + "_codes", [w], U32) for n, w in widths.items()}
         scales = {n: sbuf(n + "_scales", [w], U8) for n, w in widths.items()}
-        grouped = {n: sbuf(n + "_grouped", [PACK * widths[n]], BF16) for n in ("w1", "w3", "back")}
-        shared = sbuf("shared", [PACK * (S - BLK + FRONT)], BF16)
-        grouped["z"] = shared[:, 0 : PACK * S]
-        grouped["w2"] = shared[:, PACK * (S - BLK) : PACK * (S - BLK + FRONT)]
+        grouped = {n: sbuf(n + "_grouped", [PACK * w], BF16) for n, w in widths.items() if n not in ("x", "zb")}
+        grouped["zb"] = shared[:, 0 : 2 * HALF].bitcast(BF16)
 
         gain_rows = gain.rearrange("(p t) u -> p t u", t=PACK)
 
-        def load_weight(name, w, c0, c1):
+        def load_weight(name):
+            w, c0, c1 = pieces[name]
             nc.sync.dma_start(raw[name][:], w.rearrange("(p j) n -> p j n", j=PACK)[:, :, c0:c1])
 
         def load_gain(t):
             nc.sync.dma_start(gain_table[t][:], gain_rows[:, t, :])
 
-        def gather_gain(t):
-            nc.vector.tensor_copy(picked_gain[:, t, :], gain_table[t][:].indirect(ad_sb[:]))
+        def gather_gain(t, c0, c1):
+            nc.vector.tensor_copy(picked_gain[:, t, c0:c1], gain_table[t][:].indirect(ad_sb[:, c0 // 16 : c1 // 16]))
 
-        def quantize(name, b0, b1):
-            nc.vector.quantize_mx(
-                out=codes[name][:, b0 * BLK : b1 * BLK].bitcast(FP8X4),
-                scales=scales[name][:, b0 * BLK : b1 * BLK],
-                in_=grouped[name][:, PACK * b0 * BLK : PACK * b1 * BLK],
-            )
+        def quantize(name):
+            nc.vector.quantize_mx(out=codes[name][:].bitcast(FP8X4), scales=scales[name][:], in_=grouped[name][:])
 
-        def interleave(copy, dst, d0, src, b0, b1):
+        def interleave(copy, dst, src, c0, c1):
             copy(
-                grouped[dst][:, PACK * d0 * BLK : PACK * (d0 + b1 - b0) * BLK].rearrange("p (c i j) -> p c j i", i=4, j=PACK),
-                raw[src][:, :, b0 * BLK : b1 * BLK].rearrange("p j (c i) -> p c j i", i=4),
+                grouped[dst][:].rearrange("p (c i j) -> p c j i", i=4, j=PACK),
+                raw[src][:, :, c0:c1].rearrange("p j (c i) -> p c j i", i=4),
             )
 
         def product(acc, lhs, m, rhs, c0, c1, start, stop):
@@ -87,75 +84,95 @@ def tile_picked_slorah_none_p_kernel(tc, x_words, x_scales, w1, gain, w2, w3, of
         load_gain(0)
         for r in range(4):
             nc.sync.dma_start(xs_table[r:P:32, :].bitcast(I32), x_scales[0, r:16:4, :].bitcast(I32))
-        load_weight("w1", w1, 0, H)
+        load_weight("w1")
         load_gain(1)
         load_gain(2)
         nc.sync.dma_start(x_table[:].bitcast(I32), x_words[0].rearrange("p n t -> p (n t)").bitcast(I32))
         load_gain(3)
-        load_weight("w2", w2, 0, FRONT)
-        load_weight("w3", w3, 0, FRONT)
-        load_weight("w2_back", w2, FRONT, N)
-        load_weight("w3_back", w3, FRONT, N)
+        for name in ("w2a", "w3a", "w2b", "w3c", "w3d"):
+            load_weight(name)
 
-        gather_gain(0)
+        gather_gain(0, 0, S)
         nc.vector.tensor_copy(scales["x"][:], xs_table[:].indirect(offs_sb[:]))
         nc.scalar.copy(
             grouped["w1"][:].rearrange("p (t m j) -> p m j t", t=PACK, j=PACK),
             raw["w1"][:].rearrange("p j (m t) -> p m j t", t=PACK),
         )
-        gather_gain(1)
-        gather_gain(2)
-        quantize("w1", 0, 4)
+        gather_gain(1, 0, S)
+        gather_gain(2, 0, S)
+        quantize("w1")
         for half in range(2):
             nc.vector.tensor_copy(codes["x"][:, half * 256 : (half + 1) * 256], x_table[:].indirect(offs_sb[:, half * 16 : (half + 1) * 16]))
-        gather_gain(3)
 
-        chunks = S // BLK
-        h = [psum.tile([P, PACK, BLK], F32, name="h%d" % c) for c in range(chunks)]
-        for c in range(chunks):
+        h = {}
+
+        def hidden(c):
+            h[c] = psum.tile([P, PACK, BLK], F32, name="h%d" % c, tag="bank%d" % (c % 3))
             for t in range(PACK):
                 product(h[c][:, t, :], "w1", t, "x", c * BLK, (c + 1) * BLK, True, True)
 
-        def scale_hidden(c, engine, hidden):
+        for c in range(3):
+            hidden(c)
+
+        def scale_hidden(c):
             cols = slice(c * BLK, (c + 1) * BLK)
-            engine.tensor_tensor(
-                grouped["z"][:, PACK * c * BLK : PACK * (c + 1) * BLK].rearrange("p (c i t) -> p c t i", i=4, t=PACK),
-                hidden[:].rearrange("p t (c i) -> p c t i", i=4),
+            z = grouped["za" if c < 2 else "zb"]
+            nc.vector.tensor_tensor(
+                z[:, PACK * (c % 2) * BLK : PACK * (c % 2 + 1) * BLK].rearrange("p (c i t) -> p c t i", i=4, t=PACK),
+                h[c][:].rearrange("p t (c i) -> p c t i", i=4),
                 picked_gain[:, :, cols].rearrange("p t (c i) -> p c t i", i=4),
                 MULT,
             )
 
-        acc = [psum.tile([P, S], F32, name="acc%d" % m) for m in range(N // BLK)]
-        result = [sbuf("result%d" % m, [S], F32) for m in range(N // BLK)]
+        acc = {}
 
-        def finish(m, lhs, b, copy):
-            product(acc[m][:], lhs, b, "z", 0, S, False, True)
-            copy(result[m][:], acc[m][:])
-            nc.sync.dma_start(out[m * BLK : (m + 1) * BLK, :], result[m][:])
+        def base_path(m, half, lhs, b, bank):
+            acc[m, half] = psum.tile([P, HALF], F32, name="acc%d_%d" % (m, half), tag="bank%d" % bank)
+            product(acc[m, half][:], lhs, b, "x", half * HALF, (half + 1) * HALF, True, False)
 
-        interleave(nc.scalar.copy, "w2", 0, "w2", 0, 2)
-        interleave(nc.scalar.copy, "w2", 2, "w2", 2, 3)
-        scale_hidden(0, nc.vector, h[0])
-        scale_hidden(1, nc.vector, h[1])
-        scale_hidden(2, nc.vector, h[2])
-        quantize("z", 0, 2)
-        quantize("w2", 0, 2)
-        product(acc[0][:], "w2", 0, "x", 0, S, True, False)
-        product(acc[1][:], "w2", 1, "x", 0, S, True, False)
-        scale_hidden(3, nc.vector, h[3])
-        for b in range(3):
-            interleave(nc.scalar.copy, "w3", b, "w3", b, b + 1)
-        quantize("w3", 0, 1)
-        quantize("z", 2, 4)
-        finish(0, "w3", 0, nc.scalar.copy)
-        quantize("w3", 1, 2)
-        finish(1, "w3", 1, nc.scalar.copy)
-        quantize("w2", 2, 3)
-        product(acc[2][:], "w2", 2, "x", 0, S, True, False)
-        interleave(nc.vector.tensor_copy, "back", 0, "w2_back", 0, 1)
-        interleave(nc.vector.tensor_copy, "back", 1, "w3_back", 0, 1)
-        quantize("w3", 2, 3)
-        finish(2, "w3", 2, nc.scalar.copy)
-        quantize("back", 0, 2)
-        product(acc[3][:], "back", 0, "x", 0, S, True, False)
-        finish(3, "back", 1, nc.vector.tensor_copy)
+        early = [sbuf("early%d" % half, [2, HALF], F32) for half in range(2)]
+        late = [sbuf("late%d" % m, [2, HALF], F32) for m in range(2)]
+
+        def finish(m, half, lhs, b, copy):
+            product(acc[m, half][:], lhs, b, "zb" if half else "za", 0, HALF, False, True)
+            copy(early[half][:, m, :] if m < 2 else late[m - 2][:, half, :], acc[m, half][:])
+
+        def store_early(half):
+            nc.sync.dma_start(out[0 : 2 * BLK, half * HALF : (half + 1) * HALF].rearrange("(b p) c -> p b c", p=P), early[half][:])
+
+        def store_late(m):
+            nc.sync.dma_start(out[m * BLK : (m + 1) * BLK, :], late[m - 2][:].rearrange("p h c -> p (h c)"))
+
+        gather_gain(3, 0, HALF)
+        gather_gain(3, HALF, S)
+        scale_hidden(0)
+        hidden(3)
+        scale_hidden(1)
+        scale_hidden(2)
+        interleave(nc.scalar.copy, "w2a", "w2a", 0, 256)
+        interleave(nc.scalar.copy, "w3a", "w3a", 0, 256)
+        interleave(nc.scalar.copy, "w2b", "w2b", 0, 256)
+        quantize("w2a")
+        quantize("za")
+        quantize("w3a")
+        scale_hidden(3)
+        interleave(nc.vector.tensor_copy, "w3c", "w3c", 0, BLK)
+        quantize("zb")
+        quantize("w2b")
+        interleave(nc.vector.tensor_copy, "w3d", "w3d", 0, BLK)
+        quantize("w3c")
+        quantize("w3d")
+        for half in range(2):
+            for m in range(2):
+                base_path(m, half, "w2a", m, 4 + 2 * half + m)
+        for half in range(2):
+            for m in range(2):
+                finish(m, half, "w3a", m, nc.scalar.copy)
+            store_early(half)
+        for m in range(2, 4):
+            for half in range(2):
+                base_path(m, half, "w2b", m - 2, (3, 1, 2, 0)[2 * (m - 2) + half])
+        for m in range(2, 4):
+            finish(m, 0, "w3c" if m == 2 else "w3d", 0, nc.scalar.copy)
+            finish(m, 1, "w3c" if m == 2 else "w3d", 0, nc.vector.tensor_copy)
+            store_late(m)

@@ -39,7 +39,7 @@ def tile_picked_slorah_none_p_kernel(tc, x_words, x_scales, w1, gain, w2, w3, of
         raw = {n: sbuf(n + "_raw", [PACK, c1 - c0], F32) for n, (w, c0, c1) in pieces.items() if n != "w3a"}
         shared = sbuf("shared", [HALF + PACK * 256], F32)
         raw["w3a"] = shared[:, HALF:].rearrange("p (j n) -> p j n", j=PACK)
-        widths = {"w1": H, "w2a": 256, "w3a": 256, "w2b": 256, "w3c": BLK, "w3d": BLK, "za": HALF, "zb": HALF, "x": S}
+        widths = {"w1": H, "w2a": 256, "w3a": 256, "w2c": BLK, "w2d": BLK, "w3c": BLK, "w3d": BLK, "za": HALF, "zb": HALF, "x": S}
         codes = {n: sbuf(n + "_codes", [w], U32) for n, w in widths.items()}
         scales = {n: sbuf(n + "_scales", [w], U8) for n, w in widths.items()}
         grouped = {n: sbuf(n + "_grouped", [PACK * w], BF16) for n, w in widths.items() if n not in ("x", "zb")}
@@ -151,28 +151,31 @@ def tile_picked_slorah_none_p_kernel(tc, x_words, x_scales, w1, gain, w2, w3, of
         scale_hidden(2)
         interleave(nc.scalar.copy, "w2a", "w2a", 0, 256)
         interleave(nc.scalar.copy, "w3a", "w3a", 0, 256)
-        interleave(nc.scalar.copy, "w2b", "w2b", 0, 256)
+        interleave(nc.scalar.copy, "w2c", "w2b", 0, BLK)
+        interleave(nc.scalar.copy, "w2d", "w2b", BLK, 2 * BLK)
         quantize("w2a")
         quantize("za")
         quantize("w3a")
         scale_hidden(3)
         interleave(nc.vector.tensor_copy, "w3c", "w3c", 0, BLK)
         quantize("zb")
-        quantize("w2b")
-        interleave(nc.vector.tensor_copy, "w3d", "w3d", 0, BLK)
+        quantize("w2c")
         quantize("w3c")
+        interleave(nc.vector.tensor_copy, "w3d", "w3d", 0, BLK)
+        quantize("w2d")
         quantize("w3d")
         for half in range(2):
             for m in range(2):
                 base_path(m, half, "w2a", m, 4 + 2 * half + m)
-        for half in range(2):
-            for m in range(2):
-                finish(m, half, "w3a", m, nc.scalar.copy)
-            store_early(half)
+        for m in range(2):
+            finish(m, 0, "w3a", m, nc.scalar.copy)
+        store_early(0)
+        for m in range(2):
+            finish(m, 1, "w3a", m, nc.scalar.copy)
+            nc.sync.dma_start(out[m * BLK : (m + 1) * BLK, HALF:S], early[1][:, m, :])
         for m in range(2, 4):
             for half in range(2):
-                base_path(m, half, "w2b", m - 2, (3, 1, 2, 0)[2 * (m - 2) + half])
-        for m in range(2, 4):
+                base_path(m, half, "w2c" if m == 2 else "w2d", 0, (3, 1, 2, 0)[2 * (m - 2) + half])
             finish(m, 0, "w3c" if m == 2 else "w3d", 0, nc.scalar.copy)
             finish(m, 1, "w3c" if m == 2 else "w3d", 0, nc.vector.tensor_copy)
             store_late(m)

@@ -35,21 +35,7 @@ def tile_picked_slorah_none_p_kernel(tc, x_words, x_scales, w1, gain, w2, w3, of
         xs_table = sbuf("xs_table", [T], U8)
         gain_table = [sbuf("gain_table%d" % t, [U], F32) for t in range(PACK)]
         picked_gain = sbuf("picked_gain", [PACK, S], F32)
-        pieces = {"w1": (w1, 0, H), "w2a": (w2, 0, 256), "w3a": (w3, 0, 256), "w2b": (w2, 256, 512), "w3c": (w3, 256, 384), "w3d": (w3, 384, 512)}
-        raw = {n: sbuf(n + "_raw", [PACK, c1 - c0], F32) for n, (w, c0, c1) in pieces.items() if n != "w3a"}
-        shared = sbuf("shared", [HALF + PACK * 256], F32)
-        raw["w3a"] = shared[:, HALF:].rearrange("p (j n) -> p j n", j=PACK)
-        widths = {"w1": H, "w2a": 256, "w3a": 256, "w2c": BLK, "w2d": BLK, "w3c": BLK, "w3d": BLK, "za": HALF, "zb": HALF, "x": S}
-        codes = {n: sbuf(n + "_codes", [w], U32) for n, w in widths.items()}
-        scales = {n: sbuf(n + "_scales", [w], U8) for n, w in widths.items()}
-        grouped = {n: sbuf(n + "_grouped", [PACK * w], BF16) for n, w in widths.items() if n not in ("x", "zb")}
-        grouped["zb"] = shared[:, 0 : 2 * HALF].bitcast(BF16)
-
         gain_rows = gain.rearrange("(p t) u -> p t u", t=PACK)
-
-        def load_weight(name):
-            w, c0, c1 = pieces[name]
-            nc.sync.dma_start(raw[name][:], w.rearrange("(p j) n -> p j n", j=PACK)[:, :, c0:c1])
 
         def load_gain(t):
             nc.sync.dma_start(gain_table[t][:], gain_rows[:, t, :])
@@ -57,125 +43,173 @@ def tile_picked_slorah_none_p_kernel(tc, x_words, x_scales, w1, gain, w2, w3, of
         def gather_gain(t, c0, c1):
             nc.vector.tensor_copy(picked_gain[:, t, c0:c1], gain_table[t][:].indirect(ad_sb[:, c0 // 16 : c1 // 16]))
 
-        def quantize(name):
-            nc.vector.quantize_mx(out=codes[name][:].bitcast(FP8X4), scales=scales[name][:], in_=grouped[name][:])
+        def load_weight(dst, w, c0, c1):
+            nc.sync.dma_start(dst, w.rearrange("(p j) n -> p j n", j=PACK)[:, :, c0:c1])
 
-        def interleave(copy, dst, src, c0, c1):
-            copy(
-                grouped[dst][:].rearrange("p (c i j) -> p c j i", i=4, j=PACK),
-                raw[src][:, :, c0:c1].rearrange("p j (c i) -> p c j i", i=4),
-            )
+        def interleave(copy, dst, src):
+            copy(dst.rearrange("p (c i j) -> p c j i", i=4, j=PACK), src.rearrange("p j (c i) -> p c j i", i=4))
 
-        def product(acc, lhs, m, rhs, c0, c1, start, stop):
-            cols = slice(m * BLK, (m + 1) * BLK)
-            nc.tensor.matmul_mx(
-                out=acc,
-                lhsT=codes[lhs][:, cols].bitcast(FP8X4),
-                lhsT_scale=scales[lhs][:, cols],
-                rhs=codes[rhs][:, c0:c1].bitcast(FP8X4),
-                rhs_scale=scales[rhs][:, c0:c1],
-                start=start,
-                stop=stop,
-            )
+        def quantize(codes, scales, grouped):
+            nc.vector.quantize_mx(out=codes.bitcast(FP8X4), scales=scales, in_=grouped)
+
+        def product(acc, lhs, rhs, start, stop):
+            nc.tensor.matmul_mx(out=acc, lhsT=lhs[0].bitcast(FP8X4), lhsT_scale=lhs[1], rhs=rhs[0].bitcast(FP8X4), rhs_scale=rhs[1], start=start, stop=stop)
+
+        def mx(name, width):
+            return sbuf(name + "_codes", [width], U32), sbuf(name + "_scales", [width], U8)
+
+        def cols(operand, c0, c1):
+            return operand[0][:, c0:c1], operand[1][:, c0:c1]
+
+        shared = sbuf("shared", [3 * HALF + PACK * HALF], F32)
+        raw = {name: sbuf(name + "_raw", [PACK, width], F32)[:] for name, width in (("w2_0", BLK), ("w2_23", 2 * BLK), ("w3_2", BLK), ("w3_3", BLK))}
+        raw["w2_1"] = shared[:, HALF : 3 * HALF].rearrange("p (j n) -> p j n", j=PACK)
+        raw["w3_01"] = shared[:, 3 * HALF :].rearrange("p (j n) -> p j n", j=PACK)
+        grouped = {(w, pair): sbuf("w%d_grouped%d" % (w, pair), [2 * PACK * BLK], BF16) for w in (2, 3) for pair in range(2)}
+        w_mx = {(w, pair): mx("w%d_pair%d" % (w, pair), 2 * BLK) for w in (2, 3) for pair in range(2)}
+        z_grouped = [shared[:, 2 * HALF * half : 2 * HALF * (half + 1)].bitcast(BF16) for half in range(2)]
+        z_mx = [mx("z%d" % half, HALF) for half in range(2)]
+        w1_raw = sbuf("w1_raw", [PACK, H], F32)
+        w1_grouped = sbuf("w1_grouped", [PACK * H], BF16)
+        w1_mx = mx("w1", H)
+        x_mx = mx("x", S)
 
         nc.vector.memset(xs_table[:].bitcast(I32), 0)
-        nc.sync.dma_start(ad_sb[:], ad)
         nc.sync.dma_start(offs_sb[:], offs)
+        nc.sync.dma_start(xs_table[0:P:8, :].bitcast(I32), x_scales[0].bitcast(I32))
         load_gain(0)
-        for r in range(4):
-            nc.sync.dma_start(xs_table[r:P:32, :].bitcast(I32), x_scales[0, r:16:4, :].bitcast(I32))
-        load_weight("w1")
+        nc.sync.dma_start(ad_sb[:], ad)
+        load_weight(w1_raw[:], w1, 0, H)
         load_gain(1)
         load_gain(2)
+        picked_scales = sbuf("picked_scales", [S], U8)
+        nc.vector.tensor_copy(picked_scales[:], xs_table[:].indirect(offs_sb[:]))
+        nc.vector.tensor_copy(x_mx[1][:].bitcast(I32), picked_scales[:].bitcast(I32))
+        for r in range(1, 4):
+            nc.sync.dma_start(x_mx[1][r:P:32, :].bitcast(I32), picked_scales[8 * r : P : 32, :].bitcast(I32))
         nc.sync.dma_start(x_table[:].bitcast(I32), x_words[0].rearrange("p n t -> p (n t)").bitcast(I32))
         load_gain(3)
-        for name in ("w2a", "w3a", "w2b", "w3c", "w3d"):
-            load_weight(name)
+        load_weight(raw["w2_0"], w2, 0, BLK)
+        load_weight(raw["w2_1"], w2, BLK, 2 * BLK)
+        load_weight(raw["w3_01"], w3, 0, 2 * BLK)
+        load_weight(raw["w2_23"], w2, 2 * BLK, 4 * BLK)
+        load_weight(raw["w3_2"], w3, 2 * BLK, 3 * BLK)
+        load_weight(raw["w3_3"], w3, 3 * BLK, 4 * BLK)
 
         gather_gain(0, 0, S)
-        nc.vector.tensor_copy(scales["x"][:], xs_table[:].indirect(offs_sb[:]))
         nc.scalar.copy(
-            grouped["w1"][:].rearrange("p (t m j) -> p m j t", t=PACK, j=PACK),
-            raw["w1"][:].rearrange("p j (m t) -> p m j t", t=PACK),
+            w1_grouped[:].rearrange("p (t m j) -> p m j t", t=PACK, j=PACK),
+            w1_raw[:].rearrange("p j (m t) -> p m j t", t=PACK),
         )
         gather_gain(1, 0, S)
         gather_gain(2, 0, S)
-        quantize("w1")
+        quantize(w1_mx[0][:], w1_mx[1][:], w1_grouped[:])
         for half in range(2):
-            nc.vector.tensor_copy(codes["x"][:, half * 256 : (half + 1) * 256], x_table[:].indirect(offs_sb[:, half * 16 : (half + 1) * 16]))
+            nc.vector.tensor_copy(x_mx[0][:, half * 256 : (half + 1) * 256], x_table[:].indirect(offs_sb[:, half * 16 : (half + 1) * 16]))
 
         h = {}
 
-        def hidden(c):
-            h[c] = psum.tile([P, PACK, BLK], F32, name="h%d" % c, tag="bank%d" % (c % 3))
+        def hidden(c, bank):
+            h[c] = psum.tile([P, PACK, BLK], F32, name="h%d" % c, tag="bank%d" % bank)
             for t in range(PACK):
-                product(h[c][:, t, :], "w1", t, "x", c * BLK, (c + 1) * BLK, True, True)
+                product(h[c][:, t, :], cols(w1_mx, t * BLK, (t + 1) * BLK), cols(x_mx, c * BLK, (c + 1) * BLK), True, True)
 
-        for c in range(3):
-            hidden(c)
-
-        def scale_hidden(c):
-            cols = slice(c * BLK, (c + 1) * BLK)
-            z = grouped["za" if c < 2 else "zb"]
+        def scale_hidden(c, z):
             nc.vector.tensor_tensor(
-                z[:, PACK * (c % 2) * BLK : PACK * (c % 2 + 1) * BLK].rearrange("p (c i t) -> p c t i", i=4, t=PACK),
+                z.rearrange("p (c i t) -> p c t i", i=4, t=PACK),
                 h[c][:].rearrange("p t (c i) -> p c t i", i=4),
-                picked_gain[:, :, cols].rearrange("p t (c i) -> p c t i", i=4),
+                picked_gain[:, :, c * BLK : (c + 1) * BLK].rearrange("p t (c i) -> p c t i", i=4),
                 MULT,
             )
 
+        def z_chunk(c):
+            scale_hidden(c, z_grouped[c // 2][:, PACK * BLK * (c % 2) : PACK * BLK * (c % 2 + 1)])
+
+        def block_of(w, m):
+            return grouped[w, m // 2][:, (m % 2) * PACK * BLK : (m % 2 + 1) * PACK * BLK]
+
+
+        def stationary(w, m):
+            return cols(w_mx[w, m // 2], (m % 2) * BLK, (m % 2 + 1) * BLK)
+
+        def quantize_pair(w, pair):
+            quantize(w_mx[w, pair][0][:], w_mx[w, pair][1][:], grouped[w, pair][:])
+
+        def quantize_weight(w, m):
+            quantize(*stationary(w, m), block_of(w, m))
+
+        def quantize_z(half):
+            quantize(z_mx[half][0][:], z_mx[half][1][:], z_grouped[half])
+
         acc = {}
-
-        def base_path(m, half, lhs, b, bank):
-            acc[m, half] = psum.tile([P, HALF], F32, name="acc%d_%d" % (m, half), tag="bank%d" % bank)
-            product(acc[m, half][:], lhs, b, "x", half * HALF, (half + 1) * HALF, True, False)
-
+        late = {m: sbuf("late%d" % m, [S], F32) for m in (2, 3)}
+        staged = {(m, half): late[m][:, half * HALF : (half + 1) * HALF] for m in (2, 3) for half in range(2)}
         early = [sbuf("early%d" % half, [2, HALF], F32) for half in range(2)]
-        late = [sbuf("late%d" % m, [2, HALF], F32) for m in range(2)]
-
-        def finish(m, half, lhs, b, copy):
-            product(acc[m, half][:], lhs, b, "zb" if half else "za", 0, HALF, False, True)
-            copy(early[half][:, m, :] if m < 2 else late[m - 2][:, half, :], acc[m, half][:])
-
-        def store_early(half):
-            nc.sync.dma_start(out[0 : 2 * BLK, half * HALF : (half + 1) * HALF].rearrange("(b p) c -> p b c", p=P), early[half][:])
-
-        def store_late(m):
-            nc.sync.dma_start(out[m * BLK : (m + 1) * BLK, :], late[m - 2][:].rearrange("p h c -> p (h c)"))
-
-        gather_gain(3, 0, HALF)
-        gather_gain(3, HALF, S)
-        scale_hidden(0)
-        hidden(3)
-        scale_hidden(1)
-        scale_hidden(2)
-        interleave(nc.scalar.copy, "w2a", "w2a", 0, 256)
-        interleave(nc.scalar.copy, "w3a", "w3a", 0, 256)
-        interleave(nc.scalar.copy, "w2c", "w2b", 0, BLK)
-        interleave(nc.scalar.copy, "w2d", "w2b", BLK, 2 * BLK)
-        quantize("w2a")
-        quantize("za")
-        quantize("w3a")
-        scale_hidden(3)
-        interleave(nc.vector.tensor_copy, "w3c", "w3c", 0, BLK)
-        quantize("zb")
-        quantize("w2c")
-        quantize("w3c")
-        interleave(nc.vector.tensor_copy, "w3d", "w3d", 0, BLK)
-        quantize("w2d")
-        quantize("w3d")
         for half in range(2):
             for m in range(2):
-                base_path(m, half, "w2a", m, 4 + 2 * half + m)
+                staged[m, half] = early[half][:, m, :]
+
+        def store_first():
+            nc.sync.dma_start(out[0 : 2 * BLK, 0:HALF].rearrange("(b p) c -> p b c", p=P), early[0][:])
+
+        def base(m, half, bank):
+            acc[m, half] = psum.tile([P, HALF], F32, name="acc%d_%d" % (m, half), tag="bank%d" % bank)
+            product(acc[m, half][:], stationary(2, m), cols(x_mx, half * HALF, (half + 1) * HALF), True, False)
+
+        def finish(m, half):
+            product(acc[m, half][:], stationary(3, m), cols(z_mx[half], 0, HALF), False, True)
+
+        def empty(copy, m, half):
+            copy(staged[m, half], acc[m, half][:])
+
+        def store(m, half):
+            nc.sync.dma_start(out[m * BLK : (m + 1) * BLK, half * HALF : (half + 1) * HALF], staged[m, half])
+
+        def store_block(m):
+            nc.sync.dma_start(out[m * BLK : (m + 1) * BLK, :], late[m][:])
+
+        act, vec = nc.scalar.copy, nc.vector.tensor_copy
+
+        for c in range(3):
+            hidden(c, c)
+        gather_gain(3, 0, HALF)
+        gather_gain(3, HALF, S)
+        z_chunk(0)
+        hidden(3, 0)
+        interleave(act, block_of(2, 0), raw["w2_0"])
+        interleave(act, block_of(2, 1), raw["w2_1"])
+        interleave(act, grouped[3, 0][:], raw["w3_01"])
+        interleave(act, block_of(2, 2), raw["w2_23"][:, :, 0:BLK])
+        interleave(act, block_of(2, 3), raw["w2_23"][:, :, BLK : 2 * BLK])
+        z_chunk(1)
+        quantize_pair(2, 0)
+        z_chunk(2)
+        quantize_z(0)
+        quantize_pair(3, 0)
+        z_chunk(3)
+        interleave(vec, block_of(3, 2), raw["w3_2"])
+        quantize_z(1)
+        quantize_weight(2, 2)
+        quantize_weight(3, 2)
+        interleave(vec, block_of(3, 3), raw["w3_3"])
+        quantize_weight(2, 3)
+        quantize_weight(3, 3)
+        for half in range(2):
+            for m in range(2):
+                base(m, half, 4 + 2 * half + m)
         for m in range(2):
-            finish(m, 0, "w3a", m, nc.scalar.copy)
-        store_early(0)
+            finish(m, 0)
+            empty(act, m, 0)
+        store_first()
         for m in range(2):
-            finish(m, 1, "w3a", m, nc.scalar.copy)
-            nc.sync.dma_start(out[m * BLK : (m + 1) * BLK, HALF:S], early[1][:, m, :])
-        for m in range(2, 4):
+            finish(m, 1)
+            empty(act, m, 1)
+            store(m, 1)
+        for m in (2, 3):
             for half in range(2):
-                base_path(m, half, "w2c" if m == 2 else "w2d", 0, (3, 1, 2, 0)[2 * (m - 2) + half])
-            finish(m, 0, "w3c" if m == 2 else "w3d", 0, nc.scalar.copy)
-            finish(m, 1, "w3c" if m == 2 else "w3d", 0, nc.vector.tensor_copy)
-            store_late(m)
+                base(m, half, (3, 1, 2, 0)[2 * (m - 2) + half])
+            finish(m, 0)
+            empty(act, m, 0)
+            finish(m, 1)
+            empty(vec, m, 1)
+            store_block(m)

@@ -75,19 +75,19 @@ def tile_picked_slorah_none_p_kernel(tc, x_words, x_scales, w1, gain, w2, w3, of
         x_mx = mx("x", S)
 
         nc.vector.memset(xs_table[:].bitcast(I32), 0)
+        nc.scalar.dma_start(gain_table[0][:], gain_rows[:, 0, :])
         nc.sync.dma_start(offs_sb[:], offs)
         nc.sync.dma_start(xs_table[0:P:8, :].bitcast(I32), x_scales[0].bitcast(I32))
-        load_gain(0)
         nc.sync.dma_start(ad_sb[:], ad)
         load_weight(w1_raw[:], w1, 0, H)
         load_gain(1)
         load_gain(2)
+        nc.sync.dma_start(x_table[:].bitcast(I32), x_words[0].rearrange("p n t -> p (n t)").bitcast(I32))
         picked_scales = sbuf("picked_scales", [S], U8)
         nc.vector.tensor_copy(picked_scales[:], xs_table[:].indirect(offs_sb[:]))
         nc.vector.tensor_copy(x_mx[1][:].bitcast(I32), picked_scales[:].bitcast(I32))
         for r in range(1, 4):
             nc.sync.dma_start(x_mx[1][r:P:32, :].bitcast(I32), picked_scales[8 * r : P : 32, :].bitcast(I32))
-        nc.sync.dma_start(x_table[:].bitcast(I32), x_words[0].rearrange("p n t -> p (n t)").bitcast(I32))
         load_gain(3)
         load_weight(raw["w2_0"], w2, 0, BLK)
         load_weight(raw["w2_1"], w2, BLK, 2 * BLK)

@@ -13,6 +13,7 @@ U16 = mybir.dt.uint16
 U8 = mybir.dt.uint8
 FP8X4 = mybir.dt.float8_e4m3fn_x4
 MULT = mybir.AluOpType.mult
+COPY = mybir.ActivationFunctionType.Copy
 
 P = 128
 PACK = 4
@@ -34,14 +35,22 @@ def tile_picked_slorah_none_p_kernel(tc, x_words, x_scales, w1, gain, w2, w3, of
         x_table = sbuf("x_table", [T], U32)
         xs_table = sbuf("xs_table", [T], U8)
         gain_table = [sbuf("gain_table%d" % t, [U], F32) for t in range(PACK)]
-        picked_gain = sbuf("picked_gain", [PACK, S], F32)
+        picked_flat = sbuf("picked_flat", [PACK * S], F32)
+        picked_gain = picked_flat[:].rearrange("p (t s) -> p t s", t=PACK)
         gain_rows = gain.rearrange("(p t) u -> p t u", t=PACK)
+        act, vec = nc.scalar.copy, nc.vector.tensor_copy
 
         def load_gain(t):
             nc.sync.dma_start(gain_table[t][:], gain_rows[:, t, :])
 
-        def gather_gain(t, c0, c1):
-            nc.vector.tensor_copy(picked_gain[:, t, c0:c1], gain_table[t][:].indirect(ad_sb[:, c0 // 16 : c1 // 16]))
+        def looked_up(t, c0, c1):
+            return gain_table[t][:].indirect(ad_sb[:, c0 // 16 : c1 // 16])
+
+        def gather_gain_act(t, c0, c1):
+            nc.scalar.activation(picked_gain[:, t, c0:c1], looked_up(t, c0, c1), COPY)
+
+        def gather_gain_vec(t, c0, c1):
+            nc.vector.tensor_copy(picked_gain[:, t, c0:c1], looked_up(t, c0, c1))
 
         def load_weight(dst, w, c0, c1):
             nc.sync.dma_start(dst, w.rearrange("(p j) n -> p j n", j=PACK)[:, :, c0:c1])
@@ -49,8 +58,8 @@ def tile_picked_slorah_none_p_kernel(tc, x_words, x_scales, w1, gain, w2, w3, of
         def interleave(copy, dst, src):
             copy(dst.rearrange("p (c i j) -> p c j i", i=4, j=PACK), src.rearrange("p j (c i) -> p c j i", i=4))
 
-        def quantize(codes, scales, grouped):
-            nc.vector.quantize_mx(out=codes.bitcast(FP8X4), scales=scales, in_=grouped)
+        def quantize(operand, grouped):
+            nc.vector.quantize_mx(out=operand[0].bitcast(FP8X4), scales=operand[1], in_=grouped)
 
         def product(acc, lhs, rhs, start, stop):
             nc.tensor.matmul_mx(out=acc, lhsT=lhs[0].bitcast(FP8X4), lhsT_scale=lhs[1], rhs=rhs[0].bitcast(FP8X4), rhs_scale=rhs[1], start=start, stop=stop)
@@ -61,18 +70,31 @@ def tile_picked_slorah_none_p_kernel(tc, x_words, x_scales, w1, gain, w2, w3, of
         def cols(operand, c0, c1):
             return operand[0][:, c0:c1], operand[1][:, c0:c1]
 
-        shared = sbuf("shared", [3 * HALF + PACK * HALF], F32)
-        raw = {name: sbuf(name + "_raw", [PACK, width], F32)[:] for name, width in (("w2_0", BLK), ("w2_23", 2 * BLK), ("w3_2", BLK), ("w3_3", BLK))}
-        raw["w2_1"] = shared[:, HALF : 3 * HALF].rearrange("p (j n) -> p j n", j=PACK)
-        raw["w3_01"] = shared[:, 3 * HALF :].rearrange("p (j n) -> p j n", j=PACK)
-        grouped = {(w, pair): sbuf("w%d_grouped%d" % (w, pair), [2 * PACK * BLK], BF16) for w in (2, 3) for pair in range(2)}
-        w_mx = {(w, pair): mx("w%d_pair%d" % (w, pair), 2 * BLK) for w in (2, 3) for pair in range(2)}
-        z_grouped = [shared[:, 2 * HALF * half : 2 * HALF * (half + 1)].bitcast(BF16) for half in range(2)]
-        z_mx = [mx("z%d" % half, HALF) for half in range(2)]
+        pieces = ((2, 0, 1), (2, 1, 2), (3, 0, 2), (2, 2, 4), (3, 2, 3), (3, 3, 4))
+        spare = {(2, 0): HALF, (3, 0): HALF + BLK, (2, 2): BLK}
+        raw = {}
+        raw_piece = {}
+        raw_flat = {}
+        for w, m0, m1 in pieces:
+            front = spare.get((w, m0), 0)
+            raw_flat[w, m0] = sbuf("w%d_raw%d" % (w, m0), [front + PACK * (m1 - m0) * BLK], F32)
+            raw_piece[w, m0] = raw_flat[w, m0][:, front:].rearrange("p (j n) -> p j n", j=PACK)
+            for m in range(m0, m1):
+                raw[w, m] = raw_piece[w, m0][:, :, (m - m0) * BLK : (m - m0 + 1) * BLK]
+        z_pairs = [sbuf("z_pairs0", [2 * S], BF16)[:], raw_flat[2, 0][:, 0 : 2 * HALF].bitcast(BF16)]
+        z_grouped = [sbuf("z_grouped0", [PACK * HALF], BF16)[:], raw_flat[2, 1][:].bitcast(BF16)]
+        grouped = {block: sbuf("w%d_grouped%d" % block, [PACK * BLK], BF16)[:] for block in ((2, 0), (2, 1), (3, 0), (3, 1))}
+        for slot, block in enumerate(((2, 2), (2, 3), (3, 2))):
+            grouped.setdefault(block, raw_flat[3, 0][:, slot * HALF : (slot + 1) * HALF].bitcast(BF16))
+        grouped.setdefault((3, 3), raw_flat[2, 2][:, 0:HALF].bitcast(BF16))
+        split = 96
+        w_mx = {w: mx("w%d" % w, N) for w in (2, 3)}
+        z_mx = mx("z", S)
         w1_raw = sbuf("w1_raw", [PACK, H], F32)
         w1_grouped = sbuf("w1_grouped", [PACK * H], BF16)
         w1_mx = mx("w1", H)
         x_mx = mx("x", S)
+        picked_scales = sbuf("picked_scales", [S], U8)
 
         nc.vector.memset(xs_table[:].bitcast(I32), 0)
         nc.scalar.dma_start(gain_table[0][:], gain_rows[:, 0, :])
@@ -80,136 +102,119 @@ def tile_picked_slorah_none_p_kernel(tc, x_words, x_scales, w1, gain, w2, w3, of
         nc.sync.dma_start(xs_table[0:P:8, :].bitcast(I32), x_scales[0].bitcast(I32))
         nc.sync.dma_start(ad_sb[:], ad)
         load_weight(w1_raw[:], w1, 0, H)
-        load_gain(1)
-        load_gain(2)
         nc.sync.dma_start(x_table[:].bitcast(I32), x_words[0].rearrange("p n t -> p (n t)").bitcast(I32))
-        picked_scales = sbuf("picked_scales", [S], U8)
         nc.vector.tensor_copy(picked_scales[:], xs_table[:].indirect(offs_sb[:]))
         nc.vector.tensor_copy(x_mx[1][:].bitcast(I32), picked_scales[:].bitcast(I32))
         for r in range(1, 4):
             nc.sync.dma_start(x_mx[1][r:P:32, :].bitcast(I32), picked_scales[8 * r : P : 32, :].bitcast(I32))
-        load_gain(3)
-        load_weight(raw["w2_0"], w2, 0, BLK)
-        load_weight(raw["w2_1"], w2, BLK, 2 * BLK)
-        load_weight(raw["w3_01"], w3, 0, 2 * BLK)
-        load_weight(raw["w2_23"], w2, 2 * BLK, 4 * BLK)
-        load_weight(raw["w3_2"], w3, 2 * BLK, 3 * BLK)
-        load_weight(raw["w3_3"], w3, 3 * BLK, 4 * BLK)
+        for t in range(1, PACK):
+            load_gain(t)
+        for w, m0, m1 in pieces:
+            load_weight(raw_piece[w, m0], (w2, w3)[w - 2], m0 * BLK, m1 * BLK)
 
-        gather_gain(0, 0, S)
-        nc.scalar.copy(
+        gather_gain_act(0, 0, S)
+        vec(
             w1_grouped[:].rearrange("p (t m j) -> p m j t", t=PACK, j=PACK),
             w1_raw[:].rearrange("p j (m t) -> p m j t", t=PACK),
         )
-        gather_gain(1, 0, S)
-        gather_gain(2, 0, S)
-        quantize(w1_mx[0][:], w1_mx[1][:], w1_grouped[:])
+        quantize(cols(w1_mx, 0, H), w1_grouped[:])
         for half in range(2):
-            nc.vector.tensor_copy(x_mx[0][:, half * 256 : (half + 1) * 256], x_table[:].indirect(offs_sb[:, half * 16 : (half + 1) * 16]))
+            nc.vector.tensor_copy(x_mx[0][:, half * HALF : (half + 1) * HALF], x_table[:].indirect(offs_sb[:, half * 16 : (half + 1) * 16]))
 
         h = {}
 
-        def hidden(c, bank):
-            h[c] = psum.tile([P, PACK, BLK], F32, name="h%d" % c, tag="bank%d" % bank)
-            for t in range(PACK):
-                product(h[c][:, t, :], cols(w1_mx, t * BLK, (t + 1) * BLK), cols(x_mx, c * BLK, (c + 1) * BLK), True, True)
+        def hidden(pair, half):
+            h[pair, half] = psum.tile([P, 2, HALF], F32, name="h%d_%d" % (pair, half), tag="bank%d" % half)
+            for u in range(2):
+                t = 2 * pair + u
+                product(h[pair, half][:, u, :], cols(w1_mx, t * BLK, (t + 1) * BLK), cols(x_mx, half * HALF, (half + 1) * HALF), True, True)
 
-        def scale_hidden(c, z):
+        def scale_hidden(pair, half):
             nc.vector.tensor_tensor(
-                z.rearrange("p (c i t) -> p c t i", i=4, t=PACK),
-                h[c][:].rearrange("p t (c i) -> p c t i", i=4),
-                picked_gain[:, :, c * BLK : (c + 1) * BLK].rearrange("p t (c i) -> p c t i", i=4),
+                z_pairs[half][:, pair * S : (pair + 1) * S].rearrange("p (c i t) -> p c t i", i=4, t=2),
+                h[pair, half][:].rearrange("p t (c i) -> p c t i", i=4),
+                picked_gain[:, 2 * pair : 2 * pair + 2, half * HALF : (half + 1) * HALF].rearrange("p t (c i) -> p c t i", i=4),
                 MULT,
             )
 
-        def z_chunk(c):
-            scale_hidden(c, z_grouped[c // 2][:, PACK * BLK * (c % 2) : PACK * BLK * (c % 2 + 1)])
+        def weave(copy, word, half):
+            copy(
+                z_grouped[half].bitcast(word).rearrange("p (c u) -> p c u", u=2),
+                z_pairs[half].bitcast(word).rearrange("p (u c) -> p c u", u=2),
+            )
 
-        def block_of(w, m):
-            return grouped[w, m // 2][:, (m % 2) * PACK * BLK : (m % 2 + 1) * PACK * BLK]
-
-
-        def stationary(w, m):
-            return cols(w_mx[w, m // 2], (m % 2) * BLK, (m % 2 + 1) * BLK)
-
-        def quantize_pair(w, pair):
-            quantize(w_mx[w, pair][0][:], w_mx[w, pair][1][:], grouped[w, pair][:])
+        def group_weight(copy, w, m):
+            interleave(copy, grouped[w, m], raw[w, m])
 
         def quantize_weight(w, m):
-            quantize(*stationary(w, m), block_of(w, m))
+            quantize(cols(w_mx[w], m * BLK, (m + 1) * BLK), grouped[w, m])
 
         def quantize_z(half):
-            quantize(z_mx[half][0][:], z_mx[half][1][:], z_grouped[half])
+            quantize(cols(z_mx, half * HALF, (half + 1) * HALF), z_grouped[half])
 
         acc = {}
-        late = {m: sbuf("late%d" % m, [S], F32) for m in (2, 3)}
-        staged = {(m, half): late[m][:, half * HALF : (half + 1) * HALF] for m in (2, 3) for half in range(2)}
-        early = [sbuf("early%d" % half, [2, HALF], F32) for half in range(2)]
-        for half in range(2):
-            for m in range(2):
-                staged[m, half] = early[half][:, m, :]
+        staged = [sbuf("staged%d" % m, [S], F32) for m in range(4)]
 
-        def store_first():
-            nc.sync.dma_start(out[0 : 2 * BLK, 0:HALF].rearrange("(b p) c -> p b c", p=P), early[0][:])
+        def base(m, c0, c1, bank):
+            acc[m, c0] = psum.tile([P, c1 - c0], F32, name="acc%d_%d" % (m, c0), tag="bank%d" % bank)
+            product(acc[m, c0][:], cols(w_mx[2], m * BLK, (m + 1) * BLK), cols(x_mx, c0, c1), True, False)
 
-        def base(m, half, bank):
-            acc[m, half] = psum.tile([P, HALF], F32, name="acc%d_%d" % (m, half), tag="bank%d" % bank)
-            product(acc[m, half][:], stationary(2, m), cols(x_mx, half * HALF, (half + 1) * HALF), True, False)
+        def finish(m, c0, c1):
+            product(acc[m, c0][:], cols(w_mx[3], m * BLK, (m + 1) * BLK), cols(z_mx, c0, c1), False, True)
 
-        def finish(m, half):
-            product(acc[m, half][:], stationary(3, m), cols(z_mx[half], 0, HALF), False, True)
+        def empty(copy, m, c0, c1):
+            copy(staged[m][:, c0:c1], acc[m, c0][:])
 
-        def empty(copy, m, half):
-            copy(staged[m, half], acc[m, half][:])
+        def store(m):
+            nc.sync.dma_start(out[m * BLK : (m + 1) * BLK, :], staged[m][:])
 
-        def store(m, half):
-            nc.sync.dma_start(out[m * BLK : (m + 1) * BLK, half * HALF : (half + 1) * HALF], staged[m, half])
-
-        def store_block(m):
-            nc.sync.dma_start(out[m * BLK : (m + 1) * BLK, :], late[m][:])
-
-        act, vec = nc.scalar.copy, nc.vector.tensor_copy
-
-        for c in range(3):
-            hidden(c, c)
-        gather_gain(3, 0, HALF)
-        gather_gain(3, HALF, S)
-        z_chunk(0)
-        hidden(3, 0)
-        interleave(act, block_of(2, 0), raw["w2_0"])
-        interleave(act, block_of(2, 1), raw["w2_1"])
-        interleave(act, grouped[3, 0][:], raw["w3_01"])
-        interleave(act, block_of(2, 2), raw["w2_23"][:, :, 0:BLK])
-        interleave(act, block_of(2, 3), raw["w2_23"][:, :, BLK : 2 * BLK])
-        z_chunk(1)
-        quantize_pair(2, 0)
-        z_chunk(2)
+        hidden(0, 0)
+        hidden(0, 1)
+        gather_gain_act(1, 0, HALF)
+        gather_gain_vec(1, HALF, S)
+        scale_hidden(0, 0)
+        scale_hidden(0, 1)
+        gather_gain_act(2, 0, S)
+        hidden(1, 0)
+        hidden(1, 1)
+        gather_gain_act(3, 0, HALF)
+        gather_gain_vec(3, HALF, S)
+        scale_hidden(1, 0)
+        group_weight(act, 2, 0)
+        group_weight(act, 2, 1)
+        weave(act, U32, 0)
+        group_weight(act, 3, 0)
+        group_weight(act, 3, 1)
+        interleave(act, grouped[2, 2][:, 0 : PACK * split], raw[2, 2][:, :, 0:split])
+        quantize_weight(2, 0)
+        scale_hidden(1, 1)
+        quantize_weight(2, 1)
+        weave(vec, I32, 1)
         quantize_z(0)
-        quantize_pair(3, 0)
-        z_chunk(3)
-        interleave(vec, block_of(3, 2), raw["w3_2"])
         quantize_z(1)
-        quantize_weight(2, 2)
+        quantize_weight(3, 0)
+        group_weight(vec, 2, 3)
+        quantize_weight(3, 1)
+        interleave(vec, grouped[2, 2][:, PACK * split :], raw[2, 2][:, :, split:])
+        group_weight(vec, 3, 2)
+        quantize(cols(w_mx[2], 2 * BLK, 4 * BLK), raw_flat[3, 0][:, 0 : 2 * HALF].bitcast(BF16))
         quantize_weight(3, 2)
-        interleave(vec, block_of(3, 3), raw["w3_3"])
-        quantize_weight(2, 3)
+        group_weight(vec, 3, 3)
         quantize_weight(3, 3)
         for half in range(2):
-            for m in range(2):
-                base(m, half, 4 + 2 * half + m)
-        for m in range(2):
-            finish(m, 0)
-            empty(act, m, 0)
-        store_first()
-        for m in range(2):
-            finish(m, 1)
-            empty(act, m, 1)
-            store(m, 1)
-        for m in (2, 3):
-            for half in range(2):
-                base(m, half, (3, 1, 2, 0)[2 * (m - 2) + half])
-            finish(m, 0)
-            empty(act, m, 0)
-            finish(m, 1)
-            empty(vec, m, 1)
-            store_block(m)
+            base(0, half * HALF, (half + 1) * HALF, 2 + half)
+        base(1, 0, S, 4)
+        for half in range(2):
+            finish(0, half * HALF, (half + 1) * HALF)
+            empty(act, 0, half * HALF, (half + 1) * HALF)
+        store(0)
+        finish(1, 0, S)
+        empty(act, 1, 0, S)
+        store(1)
+        for m, width, banks in ((2, HALF, (5, 6)), (3, BLK, (7, 0, 1, 2))):
+            for part, bank in enumerate(banks):
+                base(m, part * width, (part + 1) * width, bank)
+            for part in range(len(banks)):
+                finish(m, part * width, (part + 1) * width)
+                empty((act, vec)[part % 2], m, part * width, (part + 1) * width)
+            store(m)

@@ -171,10 +171,11 @@ def tile_picked_slorah_none_p_kernel(tc, x_words, x_scales, w1, gain, w2, w3, of
         hidden(0, 0)
         hidden(0, 1)
         gather_gain_act(1, 0, HALF)
-        gather_gain_vec(1, HALF, S)
+        gather_gain_act(1, HALF, S)
         scale_hidden(0, 0)
+        gather_gain_act(2, 0, HALF)
+        gather_gain_vec(2, HALF, S)
         scale_hidden(0, 1)
-        gather_gain_act(2, 0, S)
         hidden(1, 0)
         hidden(1, 1)
         gather_gain_act(3, 0, HALF)

@@ -28,7 +28,7 @@ def tile_picked_slorah_none_p_kernel(tc, x_words, x_scales, w1, gain, w2, w3, of
         psum = ctx.enter_context(tc.psum_pool(name="psum", bufs=1))
 
         def sbuf(name, shape, dtype):
-            return keep.tile([P] + shape, dtype, name=name, align_bytes=64)
+            return keep.tile([P] + shape, dtype, name=name, align_bytes=256)
 
         offs_sb = keep.tile([P, S // 16], U16, name="offs_sb")
         ad_sb = keep.tile([P, S // 16], U16, name="ad_sb")

@@ -13,6 +13,7 @@ U16 = mybir.dt.uint16
 U8 = mybir.dt.uint8
 FP8X4 = mybir.dt.float8_e4m3fn_x4
 MULT = mybir.AluOpType.mult
+ADD = mybir.AluOpType.add
 COPY = mybir.ActivationFunctionType.Copy
 
 P = 128
@@ -39,6 +40,9 @@ def tile_picked_slorah_none_p_kernel(tc, x_words, x_scales, w1, gain, w2, w3, of
         picked_gain = picked_flat[:].rearrange("p (t s) -> p t s", t=PACK)
         gain_rows = gain.rearrange("(p t) u -> p t u", t=PACK)
         act, vec = nc.scalar.copy, nc.vector.tensor_copy
+
+        def pool_round(dst, src):
+            nc.gpsimd.tensor_scalar(dst, src, 1.0, 0.0, MULT, ADD)
 
         def load_gain(t):
             nc.sync.dma_start(gain_table[t][:], gain_rows[:, t, :])
@@ -71,23 +75,24 @@ def tile_picked_slorah_none_p_kernel(tc, x_words, x_scales, w1, gain, w2, w3, of
             return operand[0][:, c0:c1], operand[1][:, c0:c1]
 
         pieces = ((2, 0, 1), (2, 1, 2), (3, 0, 2), (2, 2, 4), (3, 2, 3), (3, 3, 4))
-        spare = {(2, 0): HALF, (3, 0): HALF + BLK, (2, 2): BLK}
+        spare = {(2, 0): HALF, (2, 1): S - BLK // 2, (3, 0): HALF + BLK, (2, 2): BLK}
+        behind = {(2, 1): S - BLK // 2}
         raw = {}
         raw_piece = {}
         raw_flat = {}
         for w, m0, m1 in pieces:
             front = spare.get((w, m0), 0)
-            raw_flat[w, m0] = sbuf("w%d_raw%d" % (w, m0), [front + PACK * (m1 - m0) * BLK], F32)
-            raw_piece[w, m0] = raw_flat[w, m0][:, front:].rearrange("p (j n) -> p j n", j=PACK)
+            raw_flat[w, m0] = sbuf("w%d_raw%d" % (w, m0), [front + PACK * (m1 - m0) * BLK + behind.get((w, m0), 0)], F32)
+            raw_piece[w, m0] = raw_flat[w, m0][:, front : front + PACK * (m1 - m0) * BLK].rearrange("p (j n) -> p j n", j=PACK)
             for m in range(m0, m1):
                 raw[w, m] = raw_piece[w, m0][:, :, (m - m0) * BLK : (m - m0 + 1) * BLK]
         z_pairs = [sbuf("z_pairs0", [2 * S], BF16)[:], raw_flat[2, 0][:, 0 : 2 * HALF].bitcast(BF16)]
-        z_grouped = [sbuf("z_grouped0", [PACK * HALF], BF16)[:], raw_flat[2, 1][:].bitcast(BF16)]
+        z_grouped = [raw_flat[2, 1][:, 0:S].bitcast(BF16), raw_flat[2, 1][:, 2 * S - BLK :].bitcast(BF16)]
         grouped = {block: sbuf("w%d_grouped%d" % block, [PACK * BLK], BF16)[:] for block in ((2, 0), (2, 1), (3, 0), (3, 1))}
         for slot, block in enumerate(((2, 2), (2, 3), (3, 2))):
             grouped.setdefault(block, raw_flat[3, 0][:, slot * HALF : (slot + 1) * HALF].bitcast(BF16))
         grouped.setdefault((3, 3), raw_flat[2, 2][:, 0:HALF].bitcast(BF16))
-        split = 96
+        split = 112
         w_mx = {w: mx("w%d" % w, N) for w in (2, 3)}
         z_mx = mx("z", S)
         w1_raw = sbuf("w1_raw", [PACK, H], F32)
@@ -170,19 +175,21 @@ def tile_picked_slorah_none_p_kernel(tc, x_words, x_scales, w1, gain, w2, w3, of
 
         hidden(0, 0)
         hidden(0, 1)
-        gather_gain_act(1, 0, HALF)
+        gather_gain_vec(1, 0, HALF)
         gather_gain_act(1, HALF, S)
         scale_hidden(0, 0)
         gather_gain_act(2, 0, HALF)
-        gather_gain_vec(2, HALF, S)
+        gather_gain_act(2, HALF, S)
         scale_hidden(0, 1)
         hidden(1, 0)
         hidden(1, 1)
-        gather_gain_act(3, 0, HALF)
-        gather_gain_vec(3, HALF, S)
+        gather_gain_vec(3, 0, HALF)
+        gather_gain_act(3, HALF, S)
         scale_hidden(1, 0)
-        group_weight(act, 2, 0)
-        group_weight(act, 2, 1)
+        interleave(act, grouped[2, 0][:, 0 : PACK * 32], raw[2, 0][:, :, 0:32])
+        interleave(pool_round, grouped[2, 0][:, PACK * 32 : PACK * 128], raw[2, 0][:, :, 32:128])
+        for c0 in (0, BLK // 2):
+            interleave(act, grouped[2, 1][:, PACK * c0 : PACK * (c0 + BLK // 2)], raw[2, 1][:, :, c0 : c0 + BLK // 2])
         weave(act, U32, 0)
         group_weight(act, 3, 0)
         group_weight(act, 3, 1)
@@ -194,9 +201,8 @@ def tile_picked_slorah_none_p_kernel(tc, x_words, x_scales, w1, gain, w2, w3, of
         quantize_z(0)
         quantize_z(1)
         quantize_weight(3, 0)
-        group_weight(vec, 2, 3)
+        interleave(vec, raw_flat[3, 0][:, 2 * split : 2 * HALF].bitcast(BF16), raw_piece[2, 2][:, :, split:])
         quantize_weight(3, 1)
-        interleave(vec, grouped[2, 2][:, PACK * split :], raw[2, 2][:, :, split:])
         group_weight(vec, 3, 2)
         quantize(cols(w_mx[2], 2 * BLK, 4 * BLK), raw_flat[3, 0][:, 0 : 2 * HALF].bitcast(BF16))
         quantize_weight(3, 2)

@@ -31,8 +31,8 @@ def tile_picked_slorah_none_p_kernel(tc, x_words, x_scales, w1, gain, w2, w3, of
         def sbuf(name, shape, dtype):
             return keep.tile([P] + shape, dtype, name=name, align_bytes=256)
 
-        offs_sb = keep.tile([P, S // 16], U16, name="offs_sb")
-        ad_sb = keep.tile([P, S // 16], U16, name="ad_sb")
+        offs_sb = sbuf("offs_sb", [S // 16], U16)
+        ad_sb = sbuf("ad_sb", [S // 16], U16)
         x_table = sbuf("x_table", [T], U32)
         xs_table = sbuf("xs_table", [T], U8)
         gain_table = [sbuf("gain_table%d" % t, [U], F32) for t in range(PACK)]
@@ -224,4 +224,8 @@ def tile_picked_slorah_none_p_kernel(tc, x_words, x_scales, w1, gain, w2, w3, of
             for part in range(len(banks)):
                 finish(m, part * width, (part + 1) * width)
                 empty((act, vec)[part % 2], m, part * width, (part + 1) * width)
-            store(m)
+                if m == 3 and part % 2 == 1:
+                    c0 = (part - 1) * width
+                    nc.sync.dma_start(out[m * BLK : (m + 1) * BLK, c0 : c0 + HALF], staged[m][:, c0 : c0 + HALF])
+            if m == 2:
+                store(m)

@@ -224,8 +224,6 @@ def tile_picked_slorah_none_p_kernel(tc, x_words, x_scales, w1, gain, w2, w3, of
             for part in range(len(banks)):
                 finish(m, part * width, (part + 1) * width)
                 empty((act, vec)[part % 2], m, part * width, (part + 1) * width)
-                if m == 3 and part % 2 == 1:
-                    c0 = (part - 1) * width
-                    nc.sync.dma_start(out[m * BLK : (m + 1) * BLK, c0 : c0 + HALF], staged[m][:, c0 : c0 + HALF])
-            if m == 2:
-                store(m)
+                done = (part + 1) * width
+                if done % HALF == 0:
+                    nc.sync.dma_start(out[m * BLK : (m + 1) * BLK, done - HALF : done], staged[m][:, done - HALF : done])

from contextlib import ExitStack

import concourse.mybir as mybir

K, T, S, N, H, U = 512, 2048, 512, 512, 512, 1024
FLOPS = 3 * 2 * 512 * 512 * 512

F32 = mybir.dt.float32
BF16 = mybir.dt.bfloat16
I32 = mybir.dt.int32
U32 = mybir.dt.uint32
U16 = mybir.dt.uint16
U8 = mybir.dt.uint8
FP8X4 = mybir.dt.float8_e4m3fn_x4
MULT = mybir.AluOpType.mult
ADD = mybir.AluOpType.add
COPY = mybir.ActivationFunctionType.Copy

P = 128
PACK = 4
BLK = 128
HALF = 256


def tile_picked_slorah_none_p_kernel(tc, x_words, x_scales, w1, gain, w2, w3, offs, ad, out):
    nc = tc.nc
    with ExitStack() as ctx:
        keep = ctx.enter_context(tc.tile_pool(name="keep", bufs=1))
        psum = ctx.enter_context(tc.psum_pool(name="psum", bufs=1))

        def sbuf(name, shape, dtype):
            return keep.tile([P] + shape, dtype, name=name, align_bytes=256)

        offs_sb = sbuf("offs_sb", [S // 16], U16)
        ad_sb = sbuf("ad_sb", [S // 16], U16)
        x_table = sbuf("x_table", [T], U32)
        xs_table = sbuf("xs_table", [T], U8)
        gain_table = [sbuf("gain_table%d" % t, [U], F32) for t in range(PACK)]
        picked_flat = sbuf("picked_flat", [PACK * S], F32)
        picked_gain = picked_flat[:].rearrange("p (t s) -> p t s", t=PACK)
        gain_rows = gain.rearrange("(p t) u -> p t u", t=PACK)
        act, vec = nc.scalar.copy, nc.vector.tensor_copy

        def pool_round(dst, src):
            nc.gpsimd.tensor_scalar(dst, src, 1.0, 0.0, MULT, ADD)

        def load_gain(t):
            nc.sync.dma_start(gain_table[t][:], gain_rows[:, t, :])

        def looked_up(t, c0, c1):
            return gain_table[t][:].indirect(ad_sb[:, c0 // 16 : c1 // 16])

        def gather_gain_act(t, c0, c1):
            nc.scalar.activation(picked_gain[:, t, c0:c1], looked_up(t, c0, c1), COPY)

        def gather_gain_vec(t, c0, c1):
            nc.vector.tensor_copy(picked_gain[:, t, c0:c1], looked_up(t, c0, c1))

        def load_weight(dst, w, c0, c1):
            nc.sync.dma_start(dst, w.rearrange("(p j) n -> p j n", j=PACK)[:, :, c0:c1])

        def interleave(copy, dst, src):
            copy(dst.rearrange("p (c i j) -> p c j i", i=4, j=PACK), src.rearrange("p j (c i) -> p c j i", i=4))

        def quantize(operand, grouped):
            nc.vector.quantize_mx(out=operand[0].bitcast(FP8X4), scales=operand[1], in_=grouped)

        def product(acc, lhs, rhs, start, stop):
            nc.tensor.matmul_mx(out=acc, lhsT=lhs[0].bitcast(FP8X4), lhsT_scale=lhs[1], rhs=rhs[0].bitcast(FP8X4), rhs_scale=rhs[1], start=start, stop=stop)

        def mx(name, width):
            return sbuf(name + "_codes", [width], U32), sbuf(name + "_scales", [width], U8)

        def cols(operand, c0, c1):
            return operand[0][:, c0:c1], operand[1][:, c0:c1]

        pieces = ((2, 0, 1), (2, 1, 2), (3, 0, 2), (2, 2, 4), (3, 2, 3), (3, 3, 4))
        spare = {(2, 0): HALF, (2, 1): S - BLK // 2, (3, 0): HALF + BLK, (2, 2): BLK}
        behind = {(2, 1): S - BLK // 2}
        raw = {}
        raw_piece = {}
        raw_flat = {}
        for w, m0, m1 in pieces:
            front = spare.get((w, m0), 0)
            raw_flat[w, m0] = sbuf("w%d_raw%d" % (w, m0), [front + PACK * (m1 - m0) * BLK + behind.get((w, m0), 0)], F32)
            raw_piece[w, m0] = raw_flat[w, m0][:, front : front + PACK * (m1 - m0) * BLK].rearrange("p (j n) -> p j n", j=PACK)
            for m in range(m0, m1):
                raw[w, m] = raw_piece[w, m0][:, :, (m - m0) * BLK : (m - m0 + 1) * BLK]
        z_pairs = [sbuf("z_pairs0", [2 * S], BF16)[:], raw_flat[2, 0][:, 0 : 2 * HALF].bitcast(BF16)]
        z_grouped = [raw_flat[2, 1][:, 0:S].bitcast(BF16), raw_flat[2, 1][:, 2 * S - BLK :].bitcast(BF16)]
        grouped = {block: sbuf("w%d_grouped%d" % block, [PACK * BLK], BF16)[:] for block in ((2, 0), (2, 1), (3, 0), (3, 1))}
        for slot, block in enumerate(((2, 2), (2, 3), (3, 2))):
            grouped.setdefault(block, raw_flat[3, 0][:, slot * HALF : (slot + 1) * HALF].bitcast(BF16))
        grouped.setdefault((3, 3), raw_flat[2, 2][:, 0:HALF].bitcast(BF16))
        split = 112
        w_mx = {w: mx("w%d" % w, N) for w in (2, 3)}
        z_mx = mx("z", S)
        w1_raw = sbuf("w1_raw", [PACK, H], F32)
        w1_grouped = sbuf("w1_grouped", [PACK * H], BF16)
        w1_mx = mx("w1", H)
        x_mx = mx("x", S)
        picked_scales = sbuf("picked_scales", [S], U8)

        nc.vector.memset(xs_table[:].bitcast(I32), 0)
        nc.scalar.dma_start(gain_table[0][:], gain_rows[:, 0, :])
        nc.sync.dma_start(offs_sb[:], offs)
        nc.sync.dma_start(xs_table[0:P:8, :].bitcast(I32), x_scales[0].bitcast(I32))
        nc.sync.dma_start(ad_sb[:], ad)
        load_weight(w1_raw[:], w1, 0, H)
        nc.sync.dma_start(x_table[:].bitcast(I32), x_words[0].rearrange("p n t -> p (n t)").bitcast(I32))
        nc.vector.tensor_copy(picked_scales[:], xs_table[:].indirect(offs_sb[:]))
        nc.vector.tensor_copy(x_mx[1][:].bitcast(I32), picked_scales[:].bitcast(I32))
        for r in range(1, 4):
            nc.sync.dma_start(x_mx[1][r:P:32, :].bitcast(I32), picked_scales[8 * r : P : 32, :].bitcast(I32))
        for t in range(1, PACK):
            load_gain(t)
        for w, m0, m1 in pieces:
            load_weight(raw_piece[w, m0], (w2, w3)[w - 2], m0 * BLK, m1 * BLK)

        gather_gain_act(0, 0, S)
        vec(
            w1_grouped[:].rearrange("p (t m j) -> p m j t", t=PACK, j=PACK),
            w1_raw[:].rearrange("p j (m t) -> p m j t", t=PACK),
        )
        quantize(cols(w1_mx, 0, H), w1_grouped[:])
        for half in range(2):
            nc.vector.tensor_copy(x_mx[0][:, half * HALF : (half + 1) * HALF], x_table[:].indirect(offs_sb[:, half * 16 : (half + 1) * 16]))

        h = {}

        def hidden(pair, half):
            h[pair, half] = psum.tile([P, 2, HALF], F32, name="h%d_%d" % (pair, half), tag="bank%d" % half)
            for u in range(2):
                t = 2 * pair + u
                product(h[pair, half][:, u, :], cols(w1_mx, t * BLK, (t + 1) * BLK), cols(x_mx, half * HALF, (half + 1) * HALF), True, True)

        def scale_hidden(pair, half):
            nc.vector.tensor_tensor(
                z_pairs[half][:, pair * S : (pair + 1) * S].rearrange("p (c i t) -> p c t i", i=4, t=2),
                h[pair, half][:].rearrange("p t (c i) -> p c t i", i=4),
                picked_gain[:, 2 * pair : 2 * pair + 2, half * HALF : (half + 1) * HALF].rearrange("p t (c i) -> p c t i", i=4),
                MULT,
            )

        def weave(copy, word, half):
            copy(
                z_grouped[half].bitcast(word).rearrange("p (c u) -> p c u", u=2),
                z_pairs[half].bitcast(word).rearrange("p (u c) -> p c u", u=2),
            )

        def group_weight(copy, w, m):
            interleave(copy, grouped[w, m], raw[w, m])

        def quantize_weight(w, m):
            quantize(cols(w_mx[w], m * BLK, (m + 1) * BLK), grouped[w, m])

        def quantize_z(half):
            quantize(cols(z_mx, half * HALF, (half + 1) * HALF), z_grouped[half])

        acc = {}
        staged = [sbuf("staged%d" % m, [S], F32) for m in range(4)]

        def base(m, c0, c1, bank):
            acc[m, c0] = psum.tile([P, c1 - c0], F32, name="acc%d_%d" % (m, c0), tag="bank%d" % bank)
            product(acc[m, c0][:], cols(w_mx[2], m * BLK, (m + 1) * BLK), cols(x_mx, c0, c1), True, False)

        def finish(m, c0, c1):
            product(acc[m, c0][:], cols(w_mx[3], m * BLK, (m + 1) * BLK), cols(z_mx, c0, c1), False, True)

        def empty(copy, m, c0, c1):
            copy(staged[m][:, c0:c1], acc[m, c0][:])

        def store(m):
            nc.sync.dma_start(out[m * BLK : (m + 1) * BLK, :], staged[m][:])

        hidden(0, 0)
        hidden(0, 1)
        gather_gain_vec(1, 0, HALF)
        gather_gain_act(1, HALF, S)
        scale_hidden(0, 0)
        gather_gain_act(2, 0, HALF)
        gather_gain_act(2, HALF, S)
        scale_hidden(0, 1)
        hidden(1, 0)
        hidden(1, 1)
        gather_gain_vec(3, 0, HALF)
        gather_gain_act(3, HALF, S)
        scale_hidden(1, 0)
        interleave(act, grouped[2, 0][:, 0 : PACK * 32], raw[2, 0][:, :, 0:32])
        interleave(pool_round, grouped[2, 0][:, PACK * 32 : PACK * 128], raw[2, 0][:, :, 32:128])
        for c0 in (0, BLK // 2):
            interleave(act, grouped[2, 1][:, PACK * c0 : PACK * (c0 + BLK // 2)], raw[2, 1][:, :, c0 : c0 + BLK // 2])
        weave(act, U32, 0)
        group_weight(act, 3, 0)
        group_weight(act, 3, 1)
        interleave(act, grouped[2, 2][:, 0 : PACK * split], raw[2, 2][:, :, 0:split])
        quantize_weight(2, 0)
        scale_hidden(1, 1)
        quantize_weight(2, 1)
        weave(vec, I32, 1)
        quantize_z(0)
        quantize_z(1)
        quantize_weight(3, 0)
        interleave(vec, raw_flat[3, 0][:, 2 * split : 2 * HALF].bitcast(BF16), raw_piece[2, 2][:, :, split:])
        quantize_weight(3, 1)
        group_weight(vec, 3, 2)
        quantize(cols(w_mx[2], 2 * BLK, 4 * BLK), raw_flat[3, 0][:, 0 : 2 * HALF].bitcast(BF16))
        quantize_weight(3, 2)
        group_weight(vec, 3, 3)
        quantize_weight(3, 3)
        for half in range(2):
            base(0, half * HALF, (half + 1) * HALF, 2 + half)
        base(1, 0, S, 4)
        for half in range(2):
            finish(0, half * HALF, (half + 1) * HALF)
            empty(act, 0, half * HALF, (half + 1) * HALF)
        store(0)
        finish(1, 0, S)
        empty(act, 1, 0, S)
        store(1)
        for m, width, banks in ((2, HALF, (5, 6)), (3, BLK, (7, 0, 1, 2))):
            for part, bank in enumerate(banks):
                base(m, part * width, (part + 1) * width, bank)
            for part in range(len(banks)):
                finish(m, part * width, (part + 1) * width)
                empty((act, vec)[part % 2], m, part * width, (part + 1) * width)
                done = (part + 1) * width
                if done % HALF == 0:
                    nc.sync.dma_start(out[m * BLK : (m + 1) * BLK, done - HALF : done], staged[m][:, done - HALF : done])
